import numpy as np, ml_dtypes
CORES = [24,25,26,27,28,29,30,31]
N = 8
BF = ml_dtypes.bfloat16
def gentries(a):
    return np.ascontiguousarray(a.reshape(8, 16, -1).transpose(0, 2, 1)).reshape(8, -1)
def gtable(e):
    e = np.asarray(e); return np.ascontiguousarray(e.reshape(8, -1, 16).transpose(0, 2, 1)).reshape(128, -1).astype(np.int32)
L, K, B, RO, CAP = 3072, 1024, 3, 12, 160
R = RO // B - 1
def pick(a, v):
    return np.take_along_axis(a, v[:, :, None, :], 3)
def moved(p, c):
    q = p + np.sum(c, axis=2)
    return np.where(q >= 16 * L, q - 16 * L, q)
def sums(C):
    return np.sum(C[..., B - 1::B], axis=2)
def splice(a, cut):
    ids = np.argsort(~cut, axis=2, kind="stable"); n = np.minimum(np.add.reduce(cut.astype(np.int64), axis=2), CAP)
    old = a.reshape(N, 8, 16, K, B); new = old.copy()
    for r in range(N):
        q = (r - 1) % N
        for g in range(8):
            m = min(int(n[r, g]), int(n[q, g]))
            new[r, g][:, ids[r, g, :m]] = old[q, g][:, ids[q, g, :m]]
    return new.reshape(N, 8, 16, L)
def parts(rng):
    x = np.abs(rng.standard_normal((N, 128, L), dtype=np.float32)) * np.exp2(rng.integers(-1, 2, (N, 128, 1)))
    return x, rng.integers(0, 16, (N, 8, 16, L)), rng.integers(0, 16 * L, (N, 8, K)), rng.integers(100, 170, (N, 8, R))
def pack(x, C, p, th):
    return {"tape": np.clip(x, 0, 4).astype(np.float32).astype(BF), "ctl": np.ascontiguousarray(C.reshape(N, 128, L)).astype(np.float32).astype(BF),
            "pos": np.stack([gtable(a) for a in p]), "th": th.astype(np.int32)}
def cols(rng, s):
    c = (s >> 4)[None, :] + (np.argsort(rng.random((16, len(s))), axis=0) < (s & 15)[None, :])
    d = (rng.random((8, len(s))) * (np.minimum(c[0::2], 15 - c[1::2]) + 1)).astype(np.int64)
    c[0::2] -= d; c[1::2] += d
    return c
def tuned(p, C, want):
    C = C.copy(); th = np.zeros((N, 8, R), np.int64)
    for t in range(RO - B):
        j = t % B; c = pick(C, p >> 4)
        C[..., j::B] = (c + C[..., j::B]) & 15
        p = moved(p, c)
        if j == B - 1:
            m = t // B; S = sums(C); D = -np.sort(-S, axis=2); w = want[m]
            a = np.take_along_axis(D, np.maximum(w - 1, 0)[..., None], 2)[..., 0]
            th[:, :, m] = np.where(w == 0, np.minimum(D[..., 0] + 1, 240), a)
            C = splice(C, S >= th[:, :, m, None])
    return th
def setup_inputs(rng):
    x, C, p, th = parts(rng); u = rng.random((N, 8, 1, L))
    C = np.where(u < 0.04, 0, np.where(u > 0.97, 15, C))
    p[..., K - 1] = 16 * L - 1; p[..., 0] = 16 * (L - 1) + rng.integers(0, 16, (N, 8))
    return pack(x, C, p, th)
def setup_inputs_spread(rng):
    x, C, p, th = parts(rng)
    x = x * np.exp2(rng.integers(-3, 4, (N, 1, L))) * (rng.random((N, 1, L)) > 0.0625)
    e = rng.choice(np.array([0.3, 1.0, 3.0]), (N, 8, 1, L), p=np.array([0.25, 0.5, 0.25]))
    C = np.minimum((16 * rng.random((N, 8, 16, L)) ** e).astype(np.int64), 15)
    p = np.where(rng.random((N, 8, K)) < 0.5, p, np.minimum((16 * L * rng.random((N, 8, K)) ** 3).astype(np.int64), 16 * L - 1))
    return pack(x, C, p, rng.integers(40, 200, (N, 8, R)))
def setup_inputs_ends(rng):
    x, C, p, th = parts(rng)
    x = np.where(rng.random(x.shape) < 0.7, np.where(rng.random(x.shape) < 0.5, 0.0, 4.0), x)
    u = rng.random((N, 8, 1, L)); C = np.where(u < 0.3, 0, np.where(u < 0.6, 15, 15 * rng.integers(0, 2, C.shape)))
    p = np.where(rng.random(p.shape) < 0.68, (16 * L - 1) * rng.integers(0, 2, p.shape), p)
    th = np.where(rng.random(th.shape) < 0.85, 240 * rng.integers(0, 2, th.shape), th)
    th[:, :, 0] = 240 * rng.integers(0, 2, (N, 8)); th[:, 0, 0] = 0; th[:, 1, 0] = 240; th[N - 1, 7, 0] = 240; th[0, 7, 0] = 240
    few = np.array([0, 1, 2, 3, K - 2, K - 1]); z = (K // 2) * B + B - 1
    for r in range(N):
        for g in range(8):
            o = (g + r) % 4
            if o == 3: continue
            C[r, g][:, z] = 0; C[r, g][:, few * B + B - 1] = 0 if o == 1 else 15
            p[r, g, few] = 16 * z + rng.integers(0, 16, len(few)); p[r, g, 4] = 0; p[r, g, K - 3] = 16 * L - 1
            if o == 1 and g > 3: th[r, g, 0] = 1
    return pack(x, C, p, th)
def setup_inputs_corners(rng):
    x, C, p, th = parts(rng)
    a = C.copy(); q = p; seen = np.zeros((N, 8, L), bool)
    for t in range(B):
        v = q >> 4; np.put_along_axis(seen, v, True, 2); c = pick(a, v)
        if t < B - 1:
            a[..., t::B] = (c + a[..., t::B]) & 15
            q = moved(q, c)
    free = ~seen[..., B - 1::B]; S = np.sum((c + C[..., B - 1::B]) & 15, axis=2)
    few = [CAP, CAP + 1, 0, CAP - 1, 1, K - 1, 2, K, 3, 256, 255]; o = int(rng.integers(0, 11))
    for r in range(N):
        for g in range(8):
            e = np.flatnonzero(free[r, g]); e = np.concatenate([e[-1:], e[:1], rng.permutation(e[1:-1])]); b = S[r, g][~free[r, g]]
            n = few[((r // 2 if g % 2 == 1 else r) + 3 * g + o) % 11]
            if n >= K - 1: lo = int(np.min(b)); m = len(e) - (K - n)
            else: lo = int(np.max(b)) + 1; m = n
            lo = min(max(lo, 1), 240); coin = rng.random(len(e)) < 0.5
            s = np.where(np.arange(len(e)) < m, np.where(coin, lo, rng.integers(lo, 241, len(e))), np.where(coin, lo - 1, rng.integers(0, lo, len(e))))
            C[r, g][:, e * B + B - 1] = (cols(rng, s) - c[r, g][:, e]) & 15
            th[r, g, 0] = lo
    th[:, 2, 1] = 240; th[:, 6, 1] = 240
    return pack(x, C, p, th)
def setup_inputs_crowd(rng):
    x, C, p, th = parts(rng)
    for r in range(N):
        for g in range(8):
            o = (g + r) % 4; at = int(rng.integers(0, 16 * L))
            if o < 2: p[r, g] = at
            if o == 1: p[r, g, K - 1] = (at + 8 * L) % (16 * L)
            if o == 2:
                own = 16 * B * np.arange(K) + rng.integers(0, 16 * B, K)
                p[r, g] = np.where(rng.random(K) < 0.5, own, rng.choice(np.array([0, 15, 16 * L - 1, 16 * (L - 1), at]), K))
            if o == 3:
                s = int(rng.integers(2, 16)); C[r, g][:, 0] = 0; C[r, g][:, B - 1] = 0; C[r, g][:, L - 1] = cols(rng, np.array([s]))[:, 0]
                p[r, g, 0] = int(rng.integers(0, 16)); p[r, g, np.array([1, K // 2, K - 1])] = 16 * L - s; p[r, g, 2] = 16 * L - s + 1; p[r, g, 3] = 16 * L - s - 1
    return pack(x, C, p, th)
def setup_inputs_calm(rng):
    x, C, p, th = parts(rng)
    for r in range(N):
        C[r, 0] = cols(rng, rng.integers(0, 4, L)); p[r, 0] = (p[r, 0] & -16) + 15 - rng.integers(0, 4, K)
        C[r, 4] = 0; C[r, 4][:, B - 1::B] = cols(rng, rng.integers(0, 4, K))
        p[r, 4] = 16 * (B * rng.integers(0, K, K) + rng.integers(0, B - 1, K)) + rng.integers(0, 16, K)
        for g in (2, 6): C[r, g] = cols(rng, rng.choice(np.array([0, 239, 240]), L))
    few = np.array([1, 0, 2, K - 1, 3, K, CAP, CAP + 1])
    o = np.arange(R)[:, None, None] + np.arange(N)[None, :, None] + 3 * np.arange(8)[None, None, :] + int(rng.integers(0, 8))
    th = tuned(p, C, few[o % 8])
    th[:, 4] = 1 + (np.arange(N)[:, None] + np.arange(R)[None, :] + int(rng.integers(0, 3))) % 3
    return pack(x, C, p, th)
def check_ranges(d):
    bad = []
    for k, lo, hi in (("tape", 0, 4), ("ctl", 0, 15), ("pos", 0, 16 * L - 1), ("th", 0, 240)):
        a = np.asarray(d[k]).astype(np.float64)
        if not (np.min(a) >= lo and np.max(a) <= hi): bad.append("range of " + k)
        elif k == "ctl" and not np.all(a == np.floor(a)): bad.append("whole numbers of ctl")
    return bad
def reference(tape, ctl, pos, th):
    X = tape.astype(np.float64).reshape(N, 8, 16, L); C = ctl.astype(np.float32).astype(np.int64).reshape(N, 8, 16, L)
    p = np.stack([gentries(a) for a in pos]).astype(np.int64); late = np.zeros((N, 8, 16, K))
    for t in range(RO):
        j = t % B; v = p >> 4; w = np.where(v == L - 1, 0, v + 1); part = ((p & 15) * 0.0625)[:, :, None, :]
        a = pick(X, v); s = a + part * (pick(X, w) - a); c = pick(C, v)
        if t > 0: late = np.roll(np.roll(before, 1, axis=0), -t, axis=1)
        X[..., j::B] = np.tanh(0.625 * s + 0.375 * late)
        C[..., j::B] = (c + C[..., j::B]) & 15
        p = moved(p, c); before = s
        if j == B - 1 and t < RO - 1:
            cut = sums(C) >= th[:, :, t // B].astype(np.int64)[:, :, None]
            X = splice(X, cut); C = splice(C, cut)
    return {"yx": X.reshape(N, 128, L).astype(np.float32), "yc": np.sum(C, axis=2).astype(np.float32),
            "yp": np.stack([np.concatenate([gtable(a >> 8), gtable(a & 255)], axis=1) for a in p]).astype(np.float32)}

def check_inputs(d):
    bad = list(check_ranges(d))
    if not bad:
        for name, y in reference(**d).items():
            for q in range(N):
                v = np.abs(np.asarray(y[q], np.float64)); s = np.sqrt(np.mean(v * v))
                if v.max() > 4 * s or s < 2.0 ** -3: bad.append('%s of rank %d is uneven or too small' % (name, q))
    return bad

@@ -1,0 +1,606 @@
+from concourse.bass import DstId, RemoteDMATransfer
+from concourse.mybir import AluOpType as ALU, ActivationFunctionType as ACT
+
+K, L, RO, CAP = 1024, 3072, 12, 160
+TL = 168
+WE = L + TL
+SP = 1088
+WW = 3 * (SP + CAP)
+F32, BF, I32, U16 = "float32", "bfloat16", "int32", "uint16"
+
+CFG = {"ad": [0, 256, 512, 768, 1024], "ms": [0, 512, 1024], "u": [0, 512, 896, 1024], "last": [0, 256, 512, 768, 1024],
+       "seed": 0, "delta": 300.0, "noise": 0.0, "x2": "V", "gx": "A", "gc": "A",
+       "split": [0] * 2 + [512] * 10, "cgv": ["1"] * 3 + [""] * 9, "upe": [0, 512, 0] + [512, 512, 0] * 2 + [512] * 3,
+       "fold": [""] * 12}
+ORDER = """
+060800020401030a070b0j0h090c0i100d0k0e110l120f0o0v0m0g0n1k1m0t1o1n1p1s1q051u1r1v200u0r130s1l15161417
+180p191g1t1b1a2930241c1h1d0q2728212c1i2a2d2b1j222f2e2k232g3i2l26252s2h3l3f3e3g2i2o3m1e3o2t2q3n3h3p1f
+3t2p3k2r2u3u412m424332443j472n482v3r3v31334546344a49404b353q4c384d4f4i36393b4g4j2j373c3a4p4q4k3d4e53
+4r4l4h4m4v4s4t50554u514n56574o5v5o5q525s585p5r5a54595u5d5b605i5t5e5f616762635g6469685j5h655c663s5k74
+725l79766a737577787a5m7c7b6b7d5n7j7h6k6c7f6e6d6g6f8j7i6l6m7e6i6n8c8e6o6s6h6j8d6p8f8m6q8k6v8i8n6r6u8r
+8p6t8l7g70718q8s8v7m90917k8g7o7n928h7s7p7l95808t7q967u9394817r82867t7v98899783848u859o87998a889a9g8b
+9h8o9p9i9n9b9ra19q9c9s9d9fa59v9e9ja69ta3a0a7b8a29ua49ka8aba9acad9laeaiafagaaahajao9mambianapatakasau
+b0avaqb1alb7b2arbcc7babdb5bebbbjb6bkbgc2blb9bhbmbqbfc1c0bnc4c3btbocac6brbpc8c5bsbub3cbcfbvc9b4cccdci
+cjchcgcsckcmcldedcdhcncodbctcucvcqdidacpd0d4crdjd1dkd7d2dddldgd3d5dpd6d8dnced9doendqdterdudvepeoele0
+dfdreme1e2eseqf3e3e5e6e4e7etf4e8dsdmf5eve9euebf6f0f1ecf9f2f7fefaeaeeedeffbegfcehggeifgfdfff8ejfhekfr
+g6flg7fifkfofsfjfug8fmgcg9gafngdghfpfqgbgegigjg3g4ftgfgkgoglh2gmgrh0gpgnfvgsgqg1g0gtg2hig5hhhghkhjho
+hqhlhmhsguhtgvhphnhui2hvhri5i0h8i1i3i4h5i6h9hah3hbi7h6hcipiriqh1inh4h7j1isj3j5j4ithdj6iviujbhej0hfio
+jej2j7jgjfj9i8jhj8jai9jdiaifibicjkidiejligiiihikijjpjciljqimjijrjjjmjsjtjujnjo
+""".replace("\n", "")
+
+SCRATCH = {
+    "rawX": ("sbuf", [128, L + 176], BF), "rawC": ("sbuf", [128, L + 176], BF),
+    "X": ("sbuf", [128, WW], F32), "C": ("sbuf", [128, WW], BF),
+    "P": ("sbuf", [128, 13 * 64], I32), "v16": ("sbuf", [128, 12 * 64], U16), "w16": ("sbuf", [128, 12 * 64], U16),
+    "lo": ("sbuf", [128, 12 * 64], I32), "ph": ("sbuf", [128, 12 * 128], BF),
+    "cb": ("sbuf", [128, 2 * K], BF), "sg": ("sbuf", [128, 2 * K], BF),
+    "a": ("sbuf", [128, 12 * K], F32), "u": ("sbuf", [128, 2 * K], F32),
+    "s": ("sbuf", [128, 12 * K], F32), "z": ("sbuf", [128, 11 * K], F32),
+    "xrow": ("sbuf", [128, 256], F32), "blk": ("sbuf", [128, 128], F32), "ki": ("sbuf", [128, 4], I32),
+    "kf": ("sbuf", [128, 8], F32), "kl0": ("sbuf", [128, 16], F32), "kl": ("sbuf", [128, 16], F32),
+    "kb": ("sbuf", [128, 16], F32), "dk": ("sbuf", [128, 16], F32),
+    "Z": ("sbuf", [128, 144], BF), "ZN": ("sbuf", [128, 144], BF), "B": ("sbuf", [128, 1024], BF), "BD": ("sbuf", [128, 128], BF),
+    "NU0": ("sbuf", [128, 128], BF), "NU": ("sbuf", [128, 128], BF), "ID": ("sbuf", [128, 128], BF),
+    "NI": ("sbuf", [128, 128], BF), "ZR": ("sbuf", [128, 256], F32), "E": ("sbuf", [128, 128], BF), "IF": ("sbuf", [128, 128], F32),
+    "thi": ("sbuf", [128, 4], I32), "thf0": ("sbuf", [128, 4], F32), "thb": ("sbuf", [128, 8], BF), "thf": ("sbuf", [128, 4], F32),
+    "cut": ("sbuf", [128, 192], BF), "inc": ("sbuf", [128, 192], BF), "MS": ("sbuf", [128, 384], F32),
+    "junk": ("sbuf", [128, 640], BF), "JS": ("sbuf", [128, 48], F32), "J16": ("sbuf", [128, 48], U16),
+    "Jb": ("sbuf", [128, 48], BF), "cmp": ("sbuf", [128, 480], BF),
+    "gl": ("sbuf", [128, 96], U16), "sl": ("sbuf", [128, 96], U16), "gid": ("sbuf", [128, 48], U16),
+    "nb": ("sbuf", [128, 12], F32), "nm": ("sbuf", [128, 12], F32), "iv": ("sbuf", [128, 48], F32),
+    "dkv": ("sbuf", [128, 48], F32), "id8": ("sbuf", [128, 48], F32), "y8": ("sbuf", [128, 48], F32),
+    "mC": ("sbuf", [128, 1440], BF), "lC": ("sbuf", [128, 1440], BF),
+    "mX": ("sbuf", [128, 1440], F32), "lX": ("sbuf", [128, 1440], F32),
+    "ycs": ("sbuf", [128, 192], F32), "pq": ("sbuf", [128, 64], F32), "pw": ("sbuf", [128, 128], I32),
+    "pi": ("sbuf", [128, 128], I32), "pf": ("sbuf", [128, 128], F32),
+    "PH": ("psum", [128, 1024], F32), "ZP": ("psum", [128, 1024], F32), "TP": ("psum", [128, 1024], F32),
+    "SM": ("psum", [128, 512], F32), "T2": ("psum", [128, 512], F32),
+}
+SEMAPHORES = (["V", "A", "P", "G", "sent", "st", "l0", "l1", "l2", "l3", "l4", "l5"]
+              + ["z%d_%d" % (t, k) for t in range(11) for k in range(4)]
+              + ["r%s%d" % (x, m) for x in "ncxy" for m in range(3)])
+
+
+JOIN = set(["J%d_%d" % (m, k) for m in range(3) for k in range(10) if k % 5]
+           + ["%s%d_%d" % (x, m, c) for x in ("gl", "sl") for m in range(3) for c in (1, 2)]
+           + ["f%d_1" % t for t in range(12)] + ["%s%d" % (x, t) for x in ("lo", "xt", "ct") for t in range(12)]
+           + ["B%d" % r for r in range(8) if r % 4] + ["ki2", "ki3", "ZR1", "NI", "pi1", "dk", "mk1", "pb15"])
+
+
+def plan(cfg):
+    ops, lastw, readers, bank = [], {}, {}, {}
+
+    def add(name, eng, fn, cost, r=(), w=(), b=(), dma=None):
+        join = name in JOIN
+        n = len(ops) - join
+        deps = set()
+        for k in r:
+            if k in lastw:
+                deps.add(lastw[k])
+        for k in w:
+            if k in lastw:
+                deps.add(lastw[k])
+            deps.update(readers.get(k, ()))
+        for k in r:
+            readers.setdefault(k, []).append(n)
+        for k in w:
+            lastw[k] = n
+            readers[k] = []
+        for k in b:
+            st = bank.setdefault(k, [eng, [], []])
+            if st[0] != eng:
+                st[0], st[2], st[1] = eng, st[1], []
+            deps.update(st[2])
+            st[1].append(n)
+        deps.discard(n)
+        if join:
+            ops[n]["fn"].append(fn)
+            ops[n]["cost"].append(cost)
+            ops[n]["deps"] = sorted(deps.union(ops[n]["deps"]))
+        else:
+            ops.append({"name": name, "eng": eng, "fn": [fn], "cost": [cost], "deps": sorted(deps), "dma": dma})
+
+    def tk(p, h0, h1):
+        return ["%s.%d" % (p, i) for i in range(h0 // 128, (h1 + 127) // 128)]
+
+    def ts(name, out, in0, s1, s2, op0, op1, n, r, w, b=(), kind="v"):
+        def fn(g, T, nx):
+            x1 = s1(T) if not isinstance(s1, (int, float)) else s1
+            if s2 is None:
+                return g.vector.tensor_scalar(out(T), in0(T), x1, None, op0)
+            x2 = s2(T) if not isinstance(s2, (int, float)) else s2
+            return g.vector.tensor_scalar(out(T), in0(T), x1, x2, op0, op1)
+        add(name, "V", fn, (kind, n), r, w, b)
+
+    def tt(name, out, in0, in1, op, n, r, w, b=(), kind="v"):
+        add(name, "V", lambda g, T, nx: g.vector.tensor_tensor(out(T), in0(T), in1(T), op), (kind, n), r, w, b)
+
+    def cp(name, eng, out, in_, n, r, w, b=(), kind="v"):
+        if eng == "V":
+            add(name, "V", lambda g, T, nx: g.vector.tensor_copy(out(T), in_(T)), (kind, n), r, w, b)
+        else:
+            act(name, out, in_, ACT.Identity, n, r, w, b, kind)
+
+    def act(name, out, in_, func, n, r, w, b=(), kind="v", **kw):
+        add(name, "A", lambda g, T, nx: g.scalar.activation(out(T), in_(T), func, **kw), (kind, n), r, w, b)
+
+    def mm(name, lst, r, w, b):
+        def fn(g, T, nx):
+            for o, l, x, s0, s1, c in lst:
+                ins = g.tensor.matmul(o(T), l(T), x(T), s0, s1)
+            return ins
+        add(name, "P", fn, ("p", sum(e[5] for e in lst)), r, w, b)
+
+    def ap(buf, a, z, step=1, p=None):
+        if p is None:
+            return lambda T: T[buf][:, a:z:step] if step != 1 else T[buf][:, a:z]
+        return lambda T: T[buf][0:p, a:z]
+
+    def ind(buf, a, z, off, c0, c1):
+        return lambda T: T[buf][:, a:z].indirect(T[off][:, c0:c1])
+
+    def load(name, q, out, in_, sem, nbytes, w):
+        add(name, q, lambda g, T, nx: (g.sync if q == "S" else g.scalar).dma_start(out(T), in_(T)), ("q", 0), (), w,
+            dma=("local", sem, nbytes))
+
+    def store(name, out, in_, nbytes, r):
+        add(name, "S", lambda g, T, nx: g.sync.dma_start(out(T), in_(T)), ("q", 0), r, (), dma=("local", "st", nbytes))
+
+    def send(name, out, in_, sem, nbytes, r, w, in2=None):
+        if in2 is None:
+            add(name, "G", lambda g, T, nx: g.remote_dma(out(T), in_(T), T.sem[sem], T.sem["sent"], nx[0], nx[1], nx[2]),
+                ("r", 0), r, w, dma=("remote", sem, nbytes))
+        else:
+            add(name, "G", lambda g, T, nx: g.remote_dma_fused(
+                [RemoteDMATransfer(dst_ids=[DstId(rid=nx[1], pnc=nx[0])], dma_engine_mask=nx[2], remote_sem=T.sem[sem],
+                                   srcs=[in_(T), in2(T)], dsts=[out(T)], alu_op=1)], local_sem=T.sem["sent"]),
+                ("r", 0), r, w, dma=("remote", sem, 2 * nbytes))
+
+    def iota(name, out, pat, cm, n, w, flt=True):
+        if flt:
+            add(name, "G", lambda g, T, nx: g.iota(out(T), pat, 0, cm, allow_small_or_imprecise_dtypes=True), ("g", n), (), w)
+        else:
+            add(name, "G", lambda g, T, nx: g.iota(out(T), pat, 0, cm), ("g", n), (), w)
+
+    Wr = [ap("Z", 15 - r, 143 - r) for r in range(16)]
+    kf = [ap("kf", i, i + 1) for i in range(8)]
+    XT = tk("X", 0, K) + ["X.t", "X.1", "X.2"]
+    CT = tk("C", 0, K) + ["C.t"]
+
+    load("ldP", "A", ap("P", 0, 64), lambda T: T.pos[:], "l0", 256, ["P0"])
+    load("ldC", "S", ap("rawC", 0, L), lambda T: T.ctl[:], "l1", 2 * L, ["rawC"])
+    load("ldX", "S", ap("rawX", 0, L), lambda T: T.tape[:], "l2", 2 * L, ["rawX"])
+    load("ldCt", "A", ap("rawC", L, L + 176), lambda T: T.ctl[:, 0:176], "l3", 352, ["rawCt"])
+    load("ldXt", "A", ap("rawX", L, L + 176), lambda T: T.tape[:, 0:176], "l4", 352, ["rawXt"])
+    load("ldT", "A", ap("thi", 0, 3, p=8), lambda T: T.th[:], "l5", 12, ["thi"])
+    iota("ki", ap("ki", 0, 1), [[0, 1]], 1, 1, ["ki0"], False)
+    iota("xrow", ap("xrow", 0, 256), [[1, 256]], 0, 256, ["xrow"])
+    iota("blk", ap("blk", 0, 128), [[16, 8], [0, 16]], 0, 128, ["blk"])
+    iota("kl0", ap("kl0", 0, 10), [[16, 10]], 1, 10, ["kl0"])
+    for i, mk in ((1, 0x70), (2, 0x77), (3, 8)):
+        ts("ki%d" % i, ap("ki", i, i + 1), ap("ki", 0, 1), mk, None, ALU.bitwise_and, None, 1, ["ki0"], ["ki%d" % i])
+    cp("kf", "V", ap("kf", 0, 4), ap("ki", 0, 4), 4, ["ki0", "ki1", "ki2", "ki3"], ["kf"])
+    ts("mk0", kf[4], kf[3], 0.0, 0.0625, ALU.is_equal, ALU.mult, 1, ["kf"], ["mk0"])
+    ts("mk1", kf[5], kf[3], 1.0 / 128, None, ALU.mult, None, 1, ["kf"], ["mk1"])
+    ts("pb15", kf[6], kf[1], 15.0, None, ALU.add, None, 1, ["kf"], ["pb15"])
+    ts("Z", ap("Z", 0, 144), ap("xrow", 0, 144), kf[6], 8.0, ALU.is_equal, ALU.mult, 144, ["xrow", "pb15"], ["Z"])
+    ts("ZN", ap("ZN", 0, 144), ap("xrow", 0, 144), kf[6], -8.0, ALU.is_equal, ALU.mult, 144, ["xrow", "pb15"], ["ZN"])
+    ts("ID", ap("ID", 0, 128), ap("xrow", 0, 128), kf[0], None, ALU.is_equal, None, 128, ["xrow", "kf"], ["ID"])
+    ts("NI", ap("NI", 0, 128), ap("xrow", 0, 128), kf[0], -1.0, ALU.is_equal, ALU.mult, 128, ["xrow", "kf"], ["NI"])
+    for r in range(8):
+        ts("B%d" % r, ap("B", 128 * r, 128 * r + 128), ap("blk", 0, 128), float(r), kf[2], ALU.add, ALU.is_equal, 128,
+           ["blk", "kf"], ["B%d" % r])
+    for h in range(2):
+        ts("ZR%d" % h, ap("ZR", 128 * h, 128 * h + 128), ap("xrow", 0, 128), kf[0], 0.6, ALU.is_equal, ALU.mult, 128,
+           ["xrow", "kf"], ["ZR%d" % h])
+    ts("BD", ap("BD", 0, 128), ap("blk", 0, 128), kf[1], None, ALU.is_equal, None, 128, ["blk", "kf"], ["BD"])
+    ts("NU0", ap("NU0", 0, 128), ap("xrow", 0, 128), kf[0], -1.0, ALU.is_lt, ALU.mult, 128, ["xrow", "kf"], ["NU0"])
+    tt("NU", ap("NU", 0, 128), ap("NU0", 0, 128), ap("BD", 0, 128), ALU.mult, 128, ["NU0", "BD"], ["NU"])
+    ts("kl", ap("kl", 0, 10), ap("kl0", 0, 10), kf[1], None, ALU.subtract, None, 10, ["kl0", "kf"], ["kl"])
+    ts("kb", ap("kb", 0, 10), ap("kl", 0, 10), 0.5, None, ALU.add, None, 10, ["kl"], ["kb"])
+    ts("dk", ap("dk", 0, 10), ap("kl", 0, 10), 8.0, 8.0 * SP, ALU.mult, ALU.add, 10, ["kl"], ["dk"])
+    ts("E", ap("E", 0, 128, p=8), ap("blk", 0, 128, p=8), 0.0625, ap("kf", 0, 1, p=8), ALU.mult, ALU.is_equal, 128,
+       ["blk", "kf"], ["E"])
+    cp("thf0", "V", ap("thf0", 0, 3, p=8), ap("thi", 0, 3, p=8), 3, ["thi"], ["thf0"])
+    cp("thb", "V", ap("thb", 0, 3, p=8), ap("thf0", 0, 3, p=8), 3, ["thf0"], ["thb"])
+    ts("cvC0", ap("C", 0, 1536), ap("rawC", 0, 1536), 0.125, None, ALU.mult, None, 1536, ["rawC"], tk("C", 0, 512), kind="h")
+    ts("cvC1", ap("C", 1536, WE), ap("rawC", 1536, WE), 0.125, None, ALU.mult, None, WE - 1536, ["rawC", "rawCt"],
+       tk("C", 512, K) + ["C.t"], kind="h")
+    for j in (1, 2):
+        add("cvX%d" % j, "G", lambda g, T, nx, j=j: g.affine_select(T["X"][:, j:WE:3], T["rawX"][:, j:WE:3], [[0, WE // 3]],
+                                                                  ALU.is_ge, 0.0, 0, 0),
+            ("g", WE // 3), ["rawX", "rawXt"], ["X.%d" % j])
+    if max(cfg["upe"]) or max(cfg["fold"]):
+        ts("IF", ap("IF", 0, 128), ap("xrow", 0, 128), kf[0], None, ALU.is_equal, None, 128, ["xrow", "kf"], ["IF"])
+
+    def lists(t):
+        c0 = 64 * t
+        src, off, rd = ap("P", c0, c0 + 64), 8.0 * t - 0.46875, ["P%d" % t]
+        ts("v%d" % t, ap("v16", c0, c0 + 64), src, 0.0625, off, ALU.mult, ALU.add, 64, rd, ["v%d" % t])
+        ts("w%d" % t, ap("w16", c0, c0 + 64), src, 0.0625, off + 1.0, ALU.mult, ALU.add, 64, rd, ["w%d" % t])
+        ts("lo%d" % t, ap("lo", c0, c0 + 64), src, 15, None, ALU.bitwise_and, None, 64, rd, ["lo%d" % t])
+        for h in range(2):
+            ts("f%d_%d" % (t, h), ap("ph", 128 * t + h, 128 * t + 128, 2), ap("lo", c0, c0 + 64), kf[4 + h], None, ALU.mult, None,
+               64, ["lo%d" % t, "mk%d" % h], ["ph%d_%d" % (t, h)])
+
+    def control(t):
+        j, o = t % 3, K * (t % 2)
+        cb, sg = "cb%d" % (t % 2), "sg%d" % (t % 2)
+        win, rd, sc = ("rawC", ["rawC", "rawCt"], 0.125) if t == 0 else ("C", CT, 1.0)
+        for h in range(2):
+            h0, h1 = 512 * h, 512 * h + 512
+            gi = ind(win, 0, WE, "v16", 64 * t + h0 // 16, 64 * t + h1 // 16)
+            if str(h) in cfg["cgv"][t]:
+                ts("c%d_%d" % (t, h), ap("cb", o + h0, o + h1), gi, sc, -1.0, ALU.mult, ALU.add, 512, rd + ["v%d" % t],
+                   tk(cb, h0, h1), kind="i")
+            else:
+                act("c%d_%d" % (t, h), ap("cb", o + h0, o + h1), gi, ACT.Identity, 512, rd + ["v%d" % t], tk(cb, h0, h1),
+                    kind="i", bias=-1.0, scale=sc)
+        sp = cfg["split"][t]
+        for h in range(2):
+            h0, h1 = 512 * h, 512 * h + 512
+            mm("to%d_%d" % (t, h), [(ap("TP", h0, h1), ap("ID", 0, 128), ap("C", 3 * h0 + j, 3 * h1, 3), True, False, 512)],
+               ["ID"] + tk("C", h0, h1), ["TP%d" % h], ["TP%d" % h])
+            mm("t%d_%d" % (t, h), [(ap("TP", h0, h1), ap("ID", 0, 128), ap("cb", o + h0, o + h1), False, True, 512)],
+               ["ID"] + tk(cb, h0, h1), ["TP%d" % h], ["TP%d" % h])
+            if h0 < sp:
+                mm("uo%d" % t, [(ap("T2", 0, 512), ap("ID", 0, 128), ap("C", j, 1536, 3), True, False, 512)],
+                   ["ID"] + tk("C", h0, h1), ["T2"], ["T2"])
+                mm("ut%d" % t, [(ap("T2", 0, 512), ap("ID", 0, 128), ap("cb", o, o + 512), False, False, 512)],
+                   ["ID"] + tk(cb, h0, h1), ["T2"], ["T2"])
+            act("sg%d_%d" % (t, h), ap("sg", o + h0, o + h1), ap("TP", h0, h1), ACT.Sign, 512, ["TP%d" % h], tk(sg, h0, h1),
+                ["TP%d" % h], bias=-0.9375)
+        mm("cs%d" % t, [(ap("SM", 0, 64), Wr[r], ap("cb", o + r, o + K, 16), r == 0, r == 15, 64) for r in range(16)],
+           ["Z"] + tk(cb, 0, K), ["SM"], ["SM"])
+        tt("p%d" % t, ap("P", 64 * t + 64, 64 * t + 128), ap("SM", 0, 64), ap("P", 64 * t, 64 * t + 64), ALU.add, 64,
+           ["SM", "P%d" % t], ["P%d" % (t + 1)], ["SM"])
+        if t < RO - 1:
+            lists(t + 1)
+        if j == 2 and t < RO - 1:
+            mm("So%d" % t, [(ap("SM", 64, 128), Wr[r], ap("C", 3 * r + 2, L, 48), r == 0, False, 64) for r in range(16)]
+               + [(ap("SM", 64, 128), Wr[r], ap("cb", o + r, o + K, 16), False, False, 64) for r in range(16)],
+               ["Z"] + tk("C", 0, K) + tk(cb, 0, K), ["SM1"], ["SM"])
+            mm("S%d" % t, [(ap("SM", 64, 128), ap("ZN", 15 - r, 143 - r), ap("sg", o + r, o + K, 16), False, r == 15, 64)
+                           for r in range(16)], ["ZN"] + tk(sg, 0, K), ["SM1"], ["SM"])
+        for h in range(2):
+            h0, h1 = 512 * h, 512 * h + 512
+            if h0 < sp:
+                src, bk = "T2", "T2"
+                mm("ac%d" % t, [(ap("T2", 0, 512), ap("NI", 0, 128), ap("sg", o, o + 512), False, True, 512)],
+                   ["NI"] + tk(sg, h0, h1), [bk], [bk])
+                cp("cn%d_%d" % (t, h), "A", ap("C", 3 * h0 + j, 3 * h1, 3), ap(src, h0, h1), 512, [bk], tk("C", h0, h1), [bk])
+                if h == 0 and t < RO - 1:
+                    cp("ct%d" % t, "A", ap("C", L + j, WE, 3), ap(src, 0, TL // 3), TL // 3, [bk], ["C.t"], [bk])
+            else:
+                bk = "TP%d" % h
+                tt("cn%d_%d" % (t, h), ap("C", 3 * h0 + j, 3 * h1, 3), ap("TP", h0, h1), ap("sg", o + h0, o + h1), ALU.subtract,
+                   512, [bk] + tk(sg, h0, h1), tk("C", h0, h1), [bk])
+                if h == 0 and t < RO - 1:
+                    tt("ct%d" % t, ap("C", L + j, WE, 3), ap("TP", 0, TL // 3), ap("sg", o, o + TL // 3), ALU.subtract,
+                       TL // 3, [bk] + tk(sg, 0, 128), ["C.t"], [bk])
+
+    def razor_control(m):
+        c64, c16, c32 = 64 * m, 16 * m, 32 * m
+        n = lambda s: "%s%d" % (s, m)
+        ts(n("cut"), ap("cut", c64, c64 + 64), ap("SM", 64, 128), ap("thf", m, m + 1), None, ALU.is_ge, None, 64,
+           ["SM1", "thf"], [n("cut")], ["SM"])
+        add(n("inc"), "V", lambda g, T, nx: g.vector.tensor_tensor_scan(T["inc"][:, c64:c64 + 64], T["cut"][:, c64:c64 + 64],
+                                                                       T["cut"][:, c64:c64 + 64], 0.0, ALU.add, ALU.max),
+            ("v", 64), [n("cut")], [n("inc")])
+        mm(n("M"), [(ap("SM", 192, 256), ap("BD", 0, 128), ap("inc", c64, c64 + 64), True, True, 64),
+                    (ap("SM", 128, 192), ap("BD", 0, 128), ap("inc", c64, c64 + 64), True, False, 64),
+                    (ap("SM", 128, 192), ap("NU", 0, 128), ap("cut", c64, c64 + 64), False, True, 64)],
+           ["BD", "NU", n("inc"), n("cut")], ["SM2"], ["SM"])
+        c128 = 128 * m
+        for kk in range(10):
+            add("J%d_%d" % (m, kk), "A", lambda g, T, nx, kk=kk: g.scalar.activation(
+                T["junk"][:, 64 * kk:64 * kk + 64], T["SM"][:, 192:256], ACT.Sign,
+                bias=T["kb"][:, kk:kk + 1], scale=-1.0, accum_out=T["JS"][:, c16 + kk:c16 + kk + 1]),
+                ("v", 84), ["SM2", "kb"], ["JS%d_%d" % (m, kk), "junk%d" % kk], ["SM"])
+        cp(n("MS"), "A", ap("MS", c128, c128 + 128), ap("SM", 128, 256), 128, ["SM2"], [n("MS")], ["SM"])
+        send(n("sn"), ap("nb", 4 * m, 4 * m + 4), ap("MS", c128 + 124, c128 + 128), n("rn"), 16, [n("MS")], [n("nb")])
+        js = ["JS%d_%d" % (m, kk) for kk in range(10)]
+        ts(n("J16"), ap("J16", c16, c16 + 10), ap("JS", c16, c16 + 10), 0.5, 32.0, ALU.mult, ALU.add, 10, js, [n("J16")])
+        act(n("Jb"), ap("Jb", c16, c16 + 10), ap("JS", c16, c16 + 10), ACT.Identity, 10, js, [n("Jb")], bias=4096.0, scale=64.0)
+        tt(n("cmp"), ap("cmp", 160 * m, 160 * m + 160), ind("MS", c128, c128 + 128, "J16", c16, c16 + 10), ap("xrow", 0, 160),
+           ALU.is_le, 160, [n("MS"), n("J16"), "xrow"], [n("cmp")], kind="i")
+        mm(n("R"), [(ap("SM", 256, 266), ap("ID", 0, 128), ap("Jb", c16, c16 + 10), True, False, 64)]
+           + [(ap("SM", 256, 266), Wr[r], ap("cmp", 160 * m + r, 160 * m + 160, 16), False, r == 15, 64) for r in range(16)],
+           ["Z", "ID", n("Jb"), n("cmp")], ["SM3"], ["SM"])
+        for c in range(3):
+            ts("gl%d_%d" % (m, c), ap("gl", c32 + 10 * c, c32 + 10 * c + 10), ap("SM", 256, 266), 0.375, float(c), ALU.mult, ALU.add,
+               10, ["SM3"], ["gl%d_%d" % (m, c)], ["SM"])
+        cp(n("id8"), "A", ap("id8", c16, c16 + 10), ap("SM", 256, 266), 10, ["SM3"], [n("id8")], ["SM"])
+        gl = ["gl%d_%d" % (m, c) for c in range(3)]
+        cp(n("gC"), cfg["gc"], ap("mC", 480 * m, 480 * m + 480), ind("C", 0, WE, "gl", c32, c32 + 30), 480, CT + gl, [n("mC")], kind="i")
+        send(n("sC"), ap("lC", 480 * m, 480 * m + 480), ap("mC", 480 * m, 480 * m + 480), n("rc"), 960, [n("mC")], [n("lC")])
+        ts(n("gid"), ap("gid", c16, c16 + 10), ap("id8", c16, c16 + 10), 0.125, float(K - 1), ALU.mult, ALU.min, 10, [n("id8")], [n("gid")])
+        tt(n("nm"), ap("nm", m, m + 1), ap("nb", 4 * m + 3, 4 * m + 4), ap("MS", c128 + 127, c128 + 128), ALU.min, 1,
+           [n("nb"), n("MS")], [n("nm")])
+        ts(n("iv"), ap("iv", c16, c16 + 10), ap("kl", 0, 10), ap("nm", m, m + 1), None, ALU.is_ge, None, 10, ["kl", n("nm")], [n("iv")])
+        tt(n("dkv"), ap("dkv", c16, c16 + 10), ap("iv", c16, c16 + 10), ap("dk", 0, 10), ALU.mult, 10, ["dk", n("iv")], [n("dkv")])
+        tt(n("y8"), ap("y8", c16, c16 + 10), ap("id8", c16, c16 + 10), ap("dkv", c16, c16 + 10), ALU.max, 10,
+           [n("id8"), n("dkv")], [n("y8")])
+        for c in range(3):
+            ts("sl%d_%d" % (m, c), ap("sl", c32 + 10 * c, c32 + 10 * c + 10), ap("y8", c16, c16 + 10), 0.375, float(c), ALU.mult, ALU.add,
+               10, [n("y8")], ["sl%d_%d" % (m, c)])
+        cp(n("xC"), "V", ind("C", 0, WW, "sl", c32, c32 + 30), ap("lC", 480 * m, 480 * m + 480), 480,
+           [n("lC")] + ["sl%d_%d" % (m, c) for c in range(3)], CT, kind="x")
+        cp(n("xCt"), "A", ap("C", L, WE), ap("C", 0, TL), TL, tk("C", 0, 128), ["C.t"])
+
+    def signal(t):
+        j, o, so = t % 3, K * (t % 2), K * t
+        m = t // 3
+        raz = j == 2 and t < RO - 1
+        a, u, s = "a%d" % t, "u%d" % (t % 2), "s%d" % t
+        win, rd = ("rawX", ["rawX", "rawXt"]) if t == 0 else ("X", XT)
+        for b in range(2):
+            mm("ph%d_%d" % (t, b), [(ap("PH", 512 * b + r, 512 * b + 512, 8), ap("B", 128 * r, 128 * r + 128),
+                                     ap("ph", 128 * t + 64 * b, 128 * t + 64 * b + 64), True, True, 64) for r in range(8)],
+               ["B%d" % r for r in range(8)] + ["ph%d_0" % t, "ph%d_1" % t], tk("PH", 512 * b, 512 * b + 512), ["PH%d" % b])
+        ms, upe = cfg["ms"], cfg["upe"][t]
+        fold = cfg["fold"][t]
+        ad = cfg["ad"]
+        for k in range(len(ad) - 1):
+            h0, h1 = ad[k], ad[k + 1]
+            l0, l1 = 64 * t + h0 // 16, 64 * t + h1 // 16
+            cp("a%d_%d" % (t, k), "A", ap("a", so + h0, so + h1), ind(win, 0, WE, "v16", l0, l1), h1 - h0, rd + ["v%d" % t],
+               tk(a, h0, h1), kind="i")
+            tt("d%d_%d" % (t, k), ap("s", so + h0, so + h1), ind(win, 0, WE, "w16", l0, l1), ap("a", so + h0, so + h1), ALU.subtract,
+               h1 - h0, rd + ["w%d" % t] + tk(a, h0, h1), tk(s, h0, h1), kind="i")
+        if t > 0:
+            sh = 16 * (t % 8)
+            for k in range(2):
+                h0, h1 = ms[k], ms[k + 1]
+                fo = str(k) in fold
+                if fo:
+                    mm("ia%d_%d" % (t, k), [(ap("ZP", h0, h1), ap("IF", 0, 128), ap("a", so + h0, so + h1), True, False, 4 * (h1 - h0))],
+                       ["IF"] + tk(a, h0, h1), tk("ZP", h0, h1), ["ZP%d" % k])
+                mm("ro%d_%d" % (t, k), [(ap("ZP", h0, h1), ap("ZR", sh, sh + 128), ap("z", so - K + h0, so - K + h1), not fo, h0 >= upe,
+                                         4 * (h1 - h0))],
+                   ["ZR0", "ZR1", "z%d_%d" % (t - 1, k)], tk("ZP", h0, h1), ["ZP%d" % k])
+        if raz:
+            cp("gX%d" % m, cfg["gx"], ap("mX", 480 * m, 480 * m + 320), ind("X", 0, WE, "gl", 32 * m, 32 * m + 20), 320,
+               XT + ["gl%d_0" % m, "gl%d_1" % m], ["mX%d" % m], kind="i")
+            send("sX%d" % m, ap("lX", 480 * m, 480 * m + 320), ap("mX", 480 * m, 480 * m + 320), "rx%d" % m, 1280,
+                 ["mX%d" % m], ["lX%d" % m])
+        if t == RO - 1:
+            ms = cfg["last"]
+        for k in range(len(ms) - 1):
+            h0, h1 = ms[k], ms[k + 1]
+            bk = ["PH%d" % (h0 // 512)]
+            if str(h0 // 512) in fold:
+                tt("m%d_%d" % (t, k), ap("s", so + h0, so + h1), ap("s", so + h0, so + h1), ap("PH", h0, h1), ALU.mult, h1 - h0,
+                   tk(s, h0, h1) + tk("PH", h0, h1), tk(s, h0, h1), bk)
+                if t < RO - 1:
+                    send("sz%d_%d" % (t, k), ap("z", so + h0, so + h1), ap("s", so + h0, so + h1), "z%d_%d" % (t, k), 4 * (h1 - h0),
+                         tk(s, h0, h1) + tk(a, h0, h1), ["z%d_%d" % (t, k)], ap("a", so + h0, so + h1))
+                continue
+            tt("m%d_%d" % (t, k), ap("PH", h0, h1), ap("s", so + h0, so + h1), ap("PH", h0, h1), ALU.mult, h1 - h0,
+               tk(s, h0, h1) + tk("PH", h0, h1), tk("PH", h0, h1), bk)
+            tt("s%d_%d" % (t, k), ap("s", so + h0, so + h1), ap("PH", h0, h1), ap("a", so + h0, so + h1), ALU.add, h1 - h0,
+               tk(a, h0, h1) + tk("PH", h0, h1), tk(s, h0, h1), bk)
+            if t < RO - 1:
+                send("sz%d_%d" % (t, k), ap("z", so + h0, so + h1), ap("s", so + h0, so + h1), "z%d_%d" % (t, k), 4 * (h1 - h0),
+                     tk(s, h0, h1), ["z%d_%d" % (t, k)])
+        uc = cfg["last"] if t == RO - 1 else cfg["u"]
+        src, sof, st = ("s", so, s) if t == 0 else ("u", o, u)
+        if t > 0:
+            for k in range(len(uc) - 1):
+                h0, h1 = uc[k], uc[k + 1]
+                if h0 < upe:
+                    if h0 % 512 == 0:
+                        mm("u%d_%d" % (t, k), [(ap("ZP", h0, h0 + 512), ap("IF", 0, 128), ap("s", so + h0, so + h0 + 512),
+                                                False, True, 2048)],
+                           ["IF"] + tk(s, h0, h0 + 512), tk("ZP", h0, h0 + 512), ["ZP%d" % (h0 // 512)])
+                    continue
+                tt("u%d_%d" % (t, k), ap("u", o + h0, o + h1), ap("ZP", h0, h1), ap("s", so + h0, so + h1), ALU.add, h1 - h0,
+                   tk(s, h0, h1) + tk("ZP", h0, h1), tk(u, h0, h1), ["ZP%d" % (h0 // 512)])
+        c0 = 480 * m + 320
+        if raz and not upe:
+            if cfg["x2"] == "V":
+                act("gY%d" % m, ap("mX", c0, c0 + 160), ind("u", o, o + K, "gid", 16 * m, 16 * m + 10), ACT.Tanh, 160,
+                    tk(u, 0, K) + ["gid%d" % m], ["mY%d" % m], kind="i", scale=0.625)
+            else:
+                act("gY%d" % m, ap("mX", c0, c0 + 160), ind("u", o, o + K, "gid", 16 * m, 16 * m + 10), ACT.Identity, 160,
+                    tk(u, 0, K) + ["gid%d" % m], ["mY%d" % m], kind="i", scale=0.625)
+            send("sY%d" % m, ap("lX", c0, c0 + 160), ap("mX", c0, c0 + 160), "ry%d" % m, 640, ["mY%d" % m], ["lY%d" % m])
+        for k in range(len(uc) - 1):
+            h0, h1 = uc[k], uc[k + 1]
+            q, qo, qt, bk = ("ZP", 0, "ZP", ["ZP%d" % (h0 // 512)]) if h0 < upe else (src, sof, st, [])
+            act("x%d_%d" % (t, k), ap("X", 3 * h0 + j, 3 * h1, 3), ap(q, qo + h0, qo + h1), ACT.Tanh, h1 - h0,
+                tk(qt, h0, h1), tk("X", h0, h1), bk, scale=0.625)
+            if k == 0 and t < RO - 1 and not raz:
+                act("xt%d" % t, ap("X", L + j, WE, 3), ap(q, qo, qo + TL // 3), ACT.Tanh, TL // 3, tk(qt, 0, 128), ["X.t"], bk,
+                    scale=0.625)
+            if t == RO - 1:
+                store("stX%d" % k, lambda T, h0=h0, h1=h1: T.yx[:, 3 * h0:3 * h1], ap("X", 3 * h0, 3 * h1), 12 * (h1 - h0),
+                      tk("X", h0, h1))
+        if raz and upe:
+            cp("gY%d" % m, "A", ap("mX", c0, c0 + 160), ind("X", 0, WE, "gl", 32 * m + 20, 32 * m + 30), 160,
+               XT + ["gl%d_2" % m], ["mY%d" % m], kind="i")
+            send("sY%d" % m, ap("lX", c0, c0 + 160), ap("mX", c0, c0 + 160), "ry%d" % m, 640, ["mY%d" % m], ["lY%d" % m])
+        if raz:
+            cp("xX%d" % m, "V", ind("X", 0, WW, "sl", 32 * m, 32 * m + 20), ap("lX", 480 * m, 480 * m + 320), 320,
+               ["lX%d" % m, "sl%d_0" % m, "sl%d_1" % m], XT, kind="x")
+            if cfg["x2"] == "V":
+                cp("xY%d" % m, "V", ind("X", 0, WW, "sl", 32 * m + 20, 32 * m + 30), ap("lX", c0, c0 + 160), 160,
+                   ["lY%d" % m, "sl%d_2" % m], XT, kind="x")
+            else:
+                act("xY%d" % m, ind("X", 0, WW, "sl", 32 * m + 20, 32 * m + 30), ap("lX", c0, c0 + 160), ACT.Tanh, 160,
+                    ["lY%d" % m, "sl%d_2" % m], XT, kind="x")
+            cp("xXt%d" % m, "A", ap("X", L, WE), ap("X", 0, TL), TL, tk("X", 0, 128), ["X.t"])
+
+    lists(0)
+    for t in range(RO):
+        control(t)
+        if t == 0:
+            mm("th", [(ap("SM", 272, 275), ap("E", 0, 128, p=8), ap("thb", 0, 3, p=8), True, True, 64)], ["E", "thb"], ["SM4"], ["SM"])
+            cp("thf", "V", ap("thf", 0, 3), ap("SM", 272, 275), 3, ["SM4"], ["thf"], ["SM"])
+        if t % 3 == 2 and t < RO - 1:
+            razor_control(t // 3)
+        signal(t)
+    mm("yc", [(ap("SM", 288, 480), Wr[r], ap("C", 192 * r, 192 * r + 192), r == 0, r == 15, 192) for r in range(16)],
+       ["Z"] + tk("C", 0, K), ["SM5"], ["SM"])
+    cp("ycs", "A", ap("ycs", 0, 192), ap("SM", 288, 480), 192, ["SM5"], ["ycs"], ["SM"])
+    store("stC", lambda T: T.yc[:], ap("ycs", 0, 192), 768, ["ycs"])
+    pe = ap("P", 64 * RO, 64 * RO + 64)
+    ts("pq", ap("pq", 0, 64), pe, 16.0 * L - 128 * RO, -16.0 * L, ALU.is_ge, ALU.mult, 64, ["P12"], ["pq"])
+    tt("pw0", ap("pw", 0, 64), pe, ap("pq", 0, 64), ALU.add, 64, ["P12", "pq"], ["pw0"])
+    ts("pw1", ap("pw", 64, 128), ap("pw", 0, 64), 128.0 * RO, None, ALU.add, None, 64, ["pw0"], ["pw1"])
+    ts("pi0", ap("pi", 0, 64), ap("pw", 64, 128), 8, None, ALU.arith_shift_right, None, 64, ["pw1"], ["pi0"])
+    ts("pi1", ap("pi", 64, 128), ap("pw", 64, 128), 255, None, ALU.bitwise_and, None, 64, ["pw1"], ["pi1"])
+    cp("pf", "V", ap("pf", 0, 128), ap("pi", 0, 128), 128, ["pi0", "pi1"], ["pf"])
+    store("stP", lambda T: T.yp[:], ap("pf", 0, 128), 512, ["pf"])
+    return ops
+
+
+MODEL = {"cyc": 1.0, "pe": 0.5, "gi": 1.56, "sx": 3.5, "fv": 50.0, "fa": 65.0, "fp": 60.0, "sem": 80.0,
+         "iss": 600.0, "isq": 100.0, "up": 1800.0, "rate": 15.0, "row": 40.0, "wake": 200.0}
+
+
+def cost(op, md):
+    return sum(cost1(op, k, n, md) for k, n in op["cost"])
+
+
+def cost1(op, k, n, md):
+    if k == "p":
+        return md["fp"] + n * md["pe"]
+    if k == "g":
+        return 150.0 + 2 * n * md["cyc"]
+    if k == "q":
+        return md["isq"]
+    if k == "r":
+        return md["iss"]
+    f = {"v": 1.0, "h": 0.5, "i": md["gi"], "x": md["sx"]}[k]
+    return (md["fv"] if op["eng"] == "V" else md["fa"]) + max(64.0, n * f) * md["cyc"]
+
+
+def xfer(op, md):
+    return 8 * (md["row"] + op["dma"][2] / md["rate"])
+
+
+def run(ops, seq, md):
+    free, done, start, dma = {}, {}, {}, [0.0]
+    for n in seq:
+        op = ops[n]
+        s = free.get(op["eng"], 0.0)
+        for x in op["deps"]:
+            s = max(s, done[x])
+        start[n] = s
+        e = s + cost(op, md)
+        free[op["eng"]] = e
+        if op["dma"]:
+            dma[0] = max(e + md["up"], dma[0]) + xfer(op, md)
+            done[n] = dma[0] + md["wake"]
+        else:
+            done[n] = e + md["sem"]
+    return start, done
+
+
+def order(ops, cfg, md):
+    n = len(ops)
+    succ = [[] for x in range(n)]
+    for i, op in enumerate(ops):
+        for x in op["deps"]:
+            succ[x].append(i)
+    lv = [0.0] * n
+    rs = cfg["seed"] * 7919 + 12345
+    for i in range(n - 1, -1, -1):
+        op = ops[i]
+        c = cost(op, md) + (md["up"] + xfer(op, md) + md["wake"] if op["dma"] else md["sem"])
+        lv[i] = c + max([lv[x] for x in succ[i]] + [0.0])
+    pr = []
+    for i in range(n):
+        rs = (rs * 1103515245 + 12345) % 2147483648
+        pr.append(lv[i] + cfg["noise"] * (rs / 2147483648.0))
+    left = [len(op["deps"]) for op in ops]
+    cand = {i: 0.0 for i in range(n) if left[i] == 0}
+    free, done, dma, seq = {}, {}, 0.0, []
+    while cand:
+        best = min(cand, key=lambda i: (max(cand[i], free.get(ops[i]["eng"], 0.0)), -pr[i]))
+        e = ops[best]["eng"]
+        lim = max(cand[best], free.get(e, 0.0)) + cfg["delta"]
+        best = max([i for i in cand if ops[i]["eng"] == e and cand[i] <= lim], key=lambda i: pr[i])
+        op = ops[best]
+        f = max(cand.pop(best), free.get(e, 0.0)) + cost(op, md)
+        free[e] = f
+        if op["dma"]:
+            dma = max(f + md["up"], dma) + xfer(op, md)
+            done[best] = dma + md["wake"]
+        else:
+            done[best] = f + md["sem"]
+        seq.append(best)
+        for x in succ[best]:
+            left[x] -= 1
+            if left[x] == 0:
+                cand[x] = max(done[y] for y in ops[x]["deps"])
+    return seq
+
+
+def waits(ops, seq):
+    count, mark, snap, clock, out = {}, {}, {}, {}, {}
+    for n in seq:
+        op = ops[n]
+        ck = clock.setdefault(op["eng"], {})
+        need = {}
+        for x in op["deps"]:
+            s, v = mark[x]
+            if need.get(s, (0, 0))[0] < v:
+                need[s] = (v, x)
+        ws = []
+        for s, (v, x) in sorted(need.items(), key=lambda e: -e[1][1]):
+            if ck.get(s, 0) < v:
+                ws.append((s, v))
+                for s2, v2 in snap[x].items():
+                    if ck.get(s2, 0) < v2:
+                        ck[s2] = v2
+        out[n] = ws
+        s, step = (op["dma"][1], 16) if op["dma"] else (op["eng"], 1)
+        count[s] = count.get(s, 0) + step
+        mark[n] = (s, count[s])
+        if op["dma"] and op["dma"][0] == "remote":
+            snap[n] = {s: count[s]}
+            count["sent"] = count.get("sent", 0) + 16
+        else:
+            snap[n] = dict(ck)
+            snap[n][s] = count[s]
+    return out, mark, count
+
+
+CACHE = {}
+
+
+def program():
+    if "p" not in CACHE:
+        ops = plan(CFG)
+        al = "0123456789abcdefghijklmnopqrstuv"
+        seq = [al.index(ORDER[i]) * 32 + al.index(ORDER[i + 1]) for i in range(0, len(ORDER), 2)] or order(ops, CFG, MODEL)
+        CACHE["p"] = (ops, seq) + waits(ops, seq)
+    return CACHE["p"]
+
+
+def emit(g, T, nx):
+    ops, seq, ws, mark, count = program()
+    qs = {"V": g.vector, "A": g.scalar, "P": g.tensor, "G": g, "S": g.sync}
+    for n in seq:
+        op = ops[n]
+        for s, v in ws[n]:
+            qs[op["eng"]].wait_ge(T.sem[s], v)
+        for fn in op["fn"]:
+            ins = fn(g, T, nx)
+        if not op["dma"]:
+            ins.then_inc(T.sem[op["eng"]], 1)
+        elif op["dma"][0] == "local":
+            ins.then_inc(T.sem[op["dma"][1]], 16)
+    for s in ("V", "A", "P", "G", "sent", "st"):
+        g.wait_ge(T.sem[s], count[s])
+
+
+def rank_program(g, core, T, topo):
+    rank = T.rank_of(core)
+    if rank is None:
+        return
+    nxt = T.cores[(rank + 1) % len(T.cores)]
+    rid, pid, se = topo.addr(nxt)
+    emit(g, T, (pid, rid, topo.mask(core, nxt)))

@@ -4,555 +4,475 @@ from concourse.mybir import AluOpType as ALU, ActivationFunctionType as ACT
 K, L, RO, CAP = 1024, 3072, 12, 160
 TL = 168
 WE = L + TL
-SP = 1088
-WW = 3 * (SP + CAP)
+NB = 76
+SP = K + CAP
+WG, WW = 3 * SP, 6 * SP
+QB = 192.0
+QS = 16 * 16 * QB
 F32, BF, I32, U16 = "float32", "bfloat16", "int32", "uint16"
+PH, TP, SR, SM = 0, 2048, 3584, 3840
 
-CFG = {"ad": [0, 256, 512, 768, 1024], "ms": [0, 512, 1024], "u": [0, 512, 896, 1024], "last": [0, 256, 512, 768, 1024],
-       "seed": 0, "delta": 300.0, "noise": 0.0, "x2": "V", "gx": "A", "gc": "A",
-       "split": [0] * 2 + [512] * 10, "cgv": ["1"] * 3 + [""] * 9, "upe": [0, 512, 0] + [512, 512, 0] * 2 + [512] * 3,
-       "fold": [""] * 12}
-ORDER = """
-060800020401030a070b0j0h090c0i100d0k0e110l120f0o0v0m0g0n1k1m0t1o1n1p1s1q051u1r1v200u0r130s1l15161417
-180p191g1t1b1a2930241c1h1d0q2728212c1i2a2d2b1j222f2e2k232g3i2l26252s2h3l3f3e3g2i2o3m1e3o2t2q3n3h3p1f
-3t2p3k2r2u3u412m424332443j472n482v3r3v31334546344a49404b353q4c384d4f4i36393b4g4j2j373c3a4p4q4k3d4e53
-4r4l4h4m4v4s4t50554u514n56574o5v5o5q525s585p5r5a54595u5d5b605i5t5e5f616762635g6469685j5h655c663s5k74
-725l79766a737577787a5m7c7b6b7d5n7j7h6k6c7f6e6d6g6f8j7i6l6m7e6i6n8c8e6o6s6h6j8d6p8f8m6q8k6v8i8n6r6u8r
-8p6t8l7g70718q8s8v7m90917k8g7o7n928h7s7p7l95808t7q967u9394817r82867t7v98899783848u859o87998a889a9g8b
-9h8o9p9i9n9b9ra19q9c9s9d9fa59v9e9ja69ta3a0a7b8a29ua49ka8aba9acad9laeaiafagaaahajao9mambianapatakasau
-b0avaqb1alb7b2arbcc7babdb5bebbbjb6bkbgc2blb9bhbmbqbfc1c0bnc4c3btbocac6brbpc8c5bsbub3cbcfbvc9b4cccdci
-cjchcgcsckcmcldedcdhcncodbctcucvcqdidacpd0d4crdjd1dkd7d2dddldgd3d5dpd6d8dnced9doendqdterdudvepeoele0
-dfdreme1e2eseqf3e3e5e6e4e7etf4e8dsdmf5eve9euebf6f0f1ecf9f2f7fefaeaeeedeffbegfcehggeifgfdfff8ejfhekfr
-g6flg7fifkfofsfjfug8fmgcg9gafngdghfpfqgbgegigjg3g4ftgfgkgoglh2gmgrh0gpgnfvgsgqg1g0gtg2hig5hhhghkhjho
-hqhlhmhsguhtgvhphnhui2hvhri5i0h8i1i3i4h5i6h9hah3hbi7h6hcipiriqh1inh4h7j1isj3j5j4ithdj6iviujbhej0hfio
-jej2j7jgjfj9i8jhj8jai9jdiaifibicjkidiejligiiihikijjpjciljqimjijrjjjmjsjtjujnjo
-""".replace("\n", "")
+A3, H2, E4 = [0, 256, 512, K], [0, 512, K], [0, 192, 512, 832, K]
+CFG = {"sp": {"s": {"ad": A3, "zb": [0, 512], "uc": H2, "ue": "VV", "ms": H2, "sz": H2},
+              "r": {"ad": A3, "zb": [0, 512], "uc": H2, "ue": "VF", "ms": H2, "sz": H2},
+              "o": {"ad": A3, "zb": [0, 512], "uc": H2, "ue": "FF", "ms": H2, "sz": H2},
+              "x": {"ad": E4, "zb": [0, 512], "uc": E4, "ue": "VVFF", "ms": E4, "sz": []}},
+       "steps": "srosrosrosrx", "slot": [0, 1, 2, 3] * 3, "xv": [""] * 12, "cv": [""] * 12, "red": (6, 7, 8, 9, 10, 11),
+       "xy": "V", "qa": (), "sc": [("C", 0, 30)], "xct": "A", "ct": "A", "xt": "A", "ms": "A"}
+
+HEAD = """
+ki ki1 kf mk kl0 ldP nil ldC xrow NI kl ZN Z v.0 NU0 ID to0.0 ldCt IF blk B0 ldX kb E w.0 ldT to1.0 BD B1 ldXt one cv2.0 x1.0 cv1.0
+tx1.0 x0.0 cn1.0 tx0.0 cn0.0 cx.0 ZR p.0 a0.0 a1.0 th0 v.1 x1.1 x0.1 a2.0 th1 f.0 NU d0.0 w.1 to0.1 ph1.0 th2 ph0.0 to1.1 tx1.1 d1.0
+q1.1 m0.0 q0.1 cx.1 tx0.1 cq.1 s0.0 f.1 p.1 v.2 th3
+"""
+CYCLE = """
+cn1+1 cn0+1 x0+2 d2+0 m1+0 q0+2 s1+0 to1+2 ro1+0 x1+2 q1+2 to0+2 tx0+2 tx1+2 ph1+1 u1+0 sz0+0 cn0+2 cn1+2 u0+0 r0+2 r1+2 t1+0 Sn+2
+Sq+2 w+2 cut+2 inc+2 M+2 sz1+0 t0+0 a0+1 a1+1 ph0+1 MS+2 d0+1 d1+1 J0+2 J1+2 m0+1 sn+2 s0+1 J16+2 sz0+1 ro0+1 cmp+2 u0+1 Jb+2 R+2 gl+2
+a2+1 ia1+1 ro1+1 d2+1 gC+2 m1+1 iv+2 y+2 u1+1 cx+2 cq+2 t0+1 t1+1 sC+2 sl+2 f+2 gid+2 p+2 w+3 a0+2 d0+2 ph1+2 sz1+1 a1+2 ph0+2 gX+2
+a2+2 ia0+2 v+3 d1+2 m0+2 xC+2 ro0+2 ia1+2 d2+2 m1+2 u0+2 ro1+2 u1+2 xCt+2 x0+3 x1+3 q0+3 to0+3 to1+3 cx+3 q1+3 gY+2 sX+2 tx0+3 sz0+2
+f+3 cq+3 t0+2 p+3 t1+2 cn0+3 w+4 v+4 f+4 xX+2 tx1+3 cn1+3 x1+4 sY+2 xY+2 ph0+3 to0+4 to1+4 x0+4 ro0+3 sz1+2 q0+4 q1+4 xXt+2 a1+3 a0+3
+cx+4 d1+3 d0+3 tx1+4 cq+4 m0+3 p+4 s0+3 v+5 tx0+4 ph1+3 a2+3
+"""
+LAST = """
+d2+0 u0+0 cn1+1 cn0+1 x1+2 x0+2 ro1+0 sz0+0 m1+0 s1+0 ph0+1 to0+2 to1+2 cx+2 t0+0 u1+0 t1+0 a0+1 ph1+1 a1+1 q0+2 w+2 q1+2 tx0+2 tx1+2
+ro0+1 a2+1 cn1+2 sz1+0 ia1+1 r1+0 d0+1 d1+1 m0+1 s0+1 Y+0 ro1+1 sz0+1 d2+1 f+2 m1+1 u0+1 u1+1 cq+2 ph0+2 ph1+2 t0+1 sz1+1 p+2 t1+1 pq
+r0+0 r0+1 pw0 pw1 a0+2 r1+1 d0+2 pi m0+2 pf s0+2 a3+2 stP a1+2 d1+2 Sn+0 Sq+0 ro0+2 a2+2 ia1+2 u0+2 m1+2 s1+2 u1+2 ro1+2 t0+2 cn0+2
+d2+2 m2+2 r1+2 u2+2 d3+2 W+1 Y+1 m3+2 r0+2 u3+2 Sn+1 Sq+1 t1+2 st0+2 W+0 t2+2 st1+2 t3+2 Sn+2 Sq+2 st2+2 ycs st3+2 stC
+"""
 
 SCRATCH = {
-    "rawX": ("sbuf", [128, L + 176], BF), "rawC": ("sbuf", [128, L + 176], BF),
-    "X": ("sbuf", [128, WW], F32), "C": ("sbuf", [128, WW], BF),
+    "rawX": ("sbuf", [128, L + 176], BF),
+    "X": ("sbuf", [128, WW], F32), "C": ("sbuf", [128, WW], BF), "Y": ("sbuf", [128, L], F32),
     "P": ("sbuf", [128, 13 * 64], I32), "v16": ("sbuf", [128, 12 * 64], U16), "w16": ("sbuf", [128, 12 * 64], U16),
     "lo": ("sbuf", [128, 12 * 64], I32), "ph": ("sbuf", [128, 12 * 128], BF),
-    "cb": ("sbuf", [128, 2 * K], BF), "sg": ("sbuf", [128, 2 * K], BF),
-    "a": ("sbuf", [128, 12 * K], F32), "u": ("sbuf", [128, 2 * K], F32),
+    "xb": ("sbuf", [128, 2 * K], BF), "qb": ("sbuf", [128, 2 * K], BF), "qn": ("sbuf", [128, 2 * K], BF),
+    "a": ("sbuf", [128, 4 * K], F32), "u": ("sbuf", [128, 2 * K], F32),
     "s": ("sbuf", [128, 12 * K], F32), "z": ("sbuf", [128, 11 * K], F32),
     "xrow": ("sbuf", [128, 256], F32), "blk": ("sbuf", [128, 128], F32), "ki": ("sbuf", [128, 4], I32),
-    "kf": ("sbuf", [128, 8], F32), "kl0": ("sbuf", [128, 16], F32), "kl": ("sbuf", [128, 16], F32),
-    "kb": ("sbuf", [128, 16], F32), "dk": ("sbuf", [128, 16], F32),
+    "kf": ("sbuf", [128, 8], F32), "kl0": ("sbuf", [128, 16], F32), "kl": ("sbuf", [128, 16], F32), "kb": ("sbuf", [128, 16], F32),
     "Z": ("sbuf", [128, 144], BF), "ZN": ("sbuf", [128, 144], BF), "B": ("sbuf", [128, 1024], BF), "BD": ("sbuf", [128, 128], BF),
     "NU0": ("sbuf", [128, 128], BF), "NU": ("sbuf", [128, 128], BF), "ID": ("sbuf", [128, 128], BF),
     "NI": ("sbuf", [128, 128], BF), "ZR": ("sbuf", [128, 256], F32), "E": ("sbuf", [128, 128], BF), "IF": ("sbuf", [128, 128], F32),
     "thi": ("sbuf", [128, 4], I32), "thf0": ("sbuf", [128, 4], F32), "thb": ("sbuf", [128, 8], BF), "thf": ("sbuf", [128, 4], F32),
-    "cut": ("sbuf", [128, 192], BF), "inc": ("sbuf", [128, 192], BF), "MS": ("sbuf", [128, 384], F32),
-    "junk": ("sbuf", [128, 640], BF), "JS": ("sbuf", [128, 48], F32), "J16": ("sbuf", [128, 48], U16),
+    "cut": ("sbuf", [128, 240], BF), "inc": ("sbuf", [128, 240], BF), "MS": ("sbuf", [128, 288], F32),
+    "junk": ("sbuf", [128, 800], BF), "JS": ("sbuf", [128, 48], F32), "J16": ("sbuf", [128, 48], U16),
     "Jb": ("sbuf", [128, 48], BF), "cmp": ("sbuf", [128, 480], BF),
     "gl": ("sbuf", [128, 96], U16), "sl": ("sbuf", [128, 96], U16), "gid": ("sbuf", [128, 48], U16),
-    "nb": ("sbuf", [128, 12], F32), "nm": ("sbuf", [128, 12], F32), "iv": ("sbuf", [128, 48], F32),
-    "dkv": ("sbuf", [128, 48], F32), "id8": ("sbuf", [128, 48], F32), "y8": ("sbuf", [128, 48], F32),
+    "nb": ("sbuf", [128, 12], F32), "iv": ("sbuf", [128, 48], F32), "y": ("sbuf", [128, 48], F32),
     "mC": ("sbuf", [128, 1440], BF), "lC": ("sbuf", [128, 1440], BF),
     "mX": ("sbuf", [128, 1440], F32), "lX": ("sbuf", [128, 1440], F32),
     "ycs": ("sbuf", [128, 192], F32), "pq": ("sbuf", [128, 64], F32), "pw": ("sbuf", [128, 128], I32),
     "pi": ("sbuf", [128, 128], I32), "pf": ("sbuf", [128, 128], F32),
-    "PH": ("psum", [128, 1024], F32), "ZP": ("psum", [128, 1024], F32), "TP": ("psum", [128, 1024], F32),
-    "SM": ("psum", [128, 512], F32), "T2": ("psum", [128, 512], F32),
+    "PS": ("psum", [128, 4096], F32),
 }
 SEMAPHORES = (["V", "A", "P", "G", "sent", "st", "l0", "l1", "l2", "l3", "l4", "l5"]
-              + ["z%d_%d" % (t, k) for t in range(11) for k in range(4)]
-              + ["r%s%d" % (x, m) for x in "ncxy" for m in range(3)])
-
-
-JOIN = set(["J%d_%d" % (m, k) for m in range(3) for k in range(10) if k % 5]
-           + ["%s%d_%d" % (x, m, c) for x in ("gl", "sl") for m in range(3) for c in (1, 2)]
-           + ["f%d_1" % t for t in range(12)] + ["%s%d" % (x, t) for x in ("lo", "xt", "ct") for t in range(12)]
-           + ["B%d" % r for r in range(8) if r % 4] + ["ki2", "ki3", "ZR1", "NI", "pi1", "dk", "mk1", "pb15"])
+              + ["%sz%d_%d" % (x, t, k) for t in range(11) for k in range(3) for x in ("", "left")]
+              + ["r%s%d" % (x, m) for x in "ncdxy" for m in range(3)])
 
 
 def plan(cfg):
-    ops, lastw, readers, bank = [], {}, {}, {}
+    ops, lastw, readers = {}, {}, {}
 
-    def add(name, eng, fn, cost, r=(), w=(), b=(), dma=None):
-        join = name in JOIN
-        n = len(ops) - join
-        deps = set()
-        for k in r:
+    def add(name, eng, fn, r=(), w=(), b=(), dma=None, grp=""):
+        op = ops.setdefault(name, {"name": name, "eng": eng, "fn": [], "deps": set(), "left": set(), "b": set(), "dma": dma, "grp": grp})
+        op["fn"].append(fn)
+        op["b"].update(b)
+        for k in list(r) + list(w):
             if k in lastw:
-                deps.add(lastw[k])
+                op["deps"].add(lastw[k])
         for k in w:
-            if k in lastw:
-                deps.add(lastw[k])
-            deps.update(readers.get(k, ()))
+            op["deps"].update(readers.get(k, ()))
+            op["left"].update(x for x in readers.get(k, ()) if ops[x]["dma"] and ops[x]["dma"][0] == "remote")
         for k in r:
-            readers.setdefault(k, []).append(n)
+            readers.setdefault(k, []).append(name)
         for k in w:
-            lastw[k] = n
+            lastw[k] = name
             readers[k] = []
-        for k in b:
-            st = bank.setdefault(k, [eng, [], []])
-            if st[0] != eng:
-                st[0], st[2], st[1] = eng, st[1], []
-            deps.update(st[2])
-            st[1].append(n)
-        deps.discard(n)
-        if join:
-            ops[n]["fn"].append(fn)
-            ops[n]["cost"].append(cost)
-            ops[n]["deps"] = sorted(deps.union(ops[n]["deps"]))
-        else:
-            ops.append({"name": name, "eng": eng, "fn": [fn], "cost": [cost], "deps": sorted(deps), "dma": dma})
+        op["deps"].discard(name)
 
     def tk(p, h0, h1):
-        return ["%s.%d" % (p, i) for i in range(h0 // 128, (h1 + 127) // 128)]
+        return ["%s.%d" % (p, i) for i in range(h0 // 64, (h1 + 63) // 64)]
 
-    def ts(name, out, in0, s1, s2, op0, op1, n, r, w, b=(), kind="v"):
+    def ts(name, out, in0, s1, s2, op0, op1, r, w, b=()):
         def fn(g, T, nx):
             x1 = s1(T) if not isinstance(s1, (int, float)) else s1
             if s2 is None:
                 return g.vector.tensor_scalar(out(T), in0(T), x1, None, op0)
             x2 = s2(T) if not isinstance(s2, (int, float)) else s2
             return g.vector.tensor_scalar(out(T), in0(T), x1, x2, op0, op1)
-        add(name, "V", fn, (kind, n), r, w, b)
+        add(name, "V", fn, r, w, b)
 
-    def tt(name, out, in0, in1, op, n, r, w, b=(), kind="v"):
-        add(name, "V", lambda g, T, nx: g.vector.tensor_tensor(out(T), in0(T), in1(T), op), (kind, n), r, w, b)
+    def tt(name, out, in0, in1, op, r, w, b=()):
+        add(name, "V", lambda g, T, nx: g.vector.tensor_tensor(out(T), in0(T), in1(T), op), r, w, b)
 
-    def cp(name, eng, out, in_, n, r, w, b=(), kind="v"):
+    def cp(name, eng, out, in_, r, w, b=(), n=0):
         if eng == "V":
-            add(name, "V", lambda g, T, nx: g.vector.tensor_copy(out(T), in_(T)), (kind, n), r, w, b)
+            add(name, "V", lambda g, T, nx: g.vector.tensor_copy(out(T), in_(T)), r, w, b)
+        elif eng == "G":
+            add(name, "G", lambda g, T, nx: g.affine_select(out(T), in_(T), [[0, n]], ALU.is_ge, 0.0, 0, 0), r, w)
         else:
-            act(name, out, in_, ACT.Identity, n, r, w, b, kind)
+            act(name, out, in_, ACT.Identity, r, w, b)
 
-    def act(name, out, in_, func, n, r, w, b=(), kind="v", **kw):
-        add(name, "A", lambda g, T, nx: g.scalar.activation(out(T), in_(T), func, **kw), (kind, n), r, w, b)
+    def act(name, out, in_, func, r, w, b=(), **kw):
+        add(name, "A", lambda g, T, nx: g.scalar.activation(out(T), in_(T), func, **kw), r, w, b)
 
-    def mm(name, lst, r, w, b):
+    def mm(name, lst, r, w, b, grp="oc"):
         def fn(g, T, nx):
-            for o, l, x, s0, s1, c in lst:
+            for o, l, x, s0, s1 in lst:
                 ins = g.tensor.matmul(o(T), l(T), x(T), s0, s1)
             return ins
-        add(name, "P", fn, ("p", sum(e[5] for e in lst)), r, w, b)
+        add(name, "P", fn, r, w, b, grp=grp)
 
     def ap(buf, a, z, step=1, p=None):
         if p is None:
             return lambda T: T[buf][:, a:z:step] if step != 1 else T[buf][:, a:z]
         return lambda T: T[buf][0:p, a:z]
 
+    def ps(a, n, step=1):
+        return ap("PS", a, a + n, step)
+
     def ind(buf, a, z, off, c0, c1):
         return lambda T: T[buf][:, a:z].indirect(T[off][:, c0:c1])
 
-    def load(name, q, out, in_, sem, nbytes, w):
-        add(name, q, lambda g, T, nx: (g.sync if q == "S" else g.scalar).dma_start(out(T), in_(T)), ("q", 0), (), w,
-            dma=("local", sem, nbytes))
+    def load(name, q, out, in_, sem, w):
+        add(name, q, lambda g, T, nx: (g.sync if q == "S" else g.scalar).dma_start(out(T), in_(T)), (), w, dma=("local", sem))
 
-    def store(name, out, in_, nbytes, r):
-        add(name, "S", lambda g, T, nx: g.sync.dma_start(out(T), in_(T)), ("q", 0), r, (), dma=("local", "st", nbytes))
+    def store(name, out, in_, r):
+        add(name, "S", lambda g, T, nx: g.sync.dma_start(out(T), in_(T)), r, (), dma=("local", "st"))
 
-    def send(name, out, in_, sem, nbytes, r, w, in2=None):
+    def send(name, out, in_, sem, r, w, in2=None):
         if in2 is None:
             add(name, "G", lambda g, T, nx: g.remote_dma(out(T), in_(T), T.sem[sem], T.sem["sent"], nx[0], nx[1], nx[2]),
-                ("r", 0), r, w, dma=("remote", sem, nbytes))
+                r, w, dma=("remote", sem, "sent"))
         else:
             add(name, "G", lambda g, T, nx: g.remote_dma_fused(
                 [RemoteDMATransfer(dst_ids=[DstId(rid=nx[1], pnc=nx[0])], dma_engine_mask=nx[2], remote_sem=T.sem[sem],
-                                   srcs=[in_(T), in2(T)], dsts=[out(T)], alu_op=1)], local_sem=T.sem["sent"]),
-                ("r", 0), r, w, dma=("remote", sem, 2 * nbytes))
+                                   srcs=[in_(T), in2(T)], dsts=[out(T)], alu_op=1)], local_sem=T.sem["left" + sem]),
+                r, w, dma=("remote", sem, "left" + sem))
 
-    def iota(name, out, pat, cm, n, w, flt=True):
+    def iota(name, out, pat, cm, w, flt=True):
         if flt:
-            add(name, "G", lambda g, T, nx: g.iota(out(T), pat, 0, cm, allow_small_or_imprecise_dtypes=True), ("g", n), (), w)
+            add(name, "G", lambda g, T, nx: g.iota(out(T), pat, 0, cm, allow_small_or_imprecise_dtypes=True), (), w)
         else:
-            add(name, "G", lambda g, T, nx: g.iota(out(T), pat, 0, cm), ("g", n), (), w)
+            add(name, "G", lambda g, T, nx: g.iota(out(T), pat, 0, cm), (), w)
 
     Wr = [ap("Z", 15 - r, 143 - r) for r in range(16)]
+    Wn = [ap("ZN", 15 - r, 143 - r) for r in range(16)]
+    ID, NI, IF, BD, NU = [ap(x, 0, 128) for x in ("ID", "NI", "IF", "BD", "NU")]
     kf = [ap("kf", i, i + 1) for i in range(8)]
-    XT = tk("X", 0, K) + ["X.t", "X.1", "X.2"]
-    CT = tk("C", 0, K) + ["C.t"]
+    XT = tk("X", 0, K) + ["X.t", "X.p1", "X.p2", "X.s"]
+    CP = [["C%d.0" % j, "C%d.1" % j] for j in range(3)]
+    CT = CP[0] + CP[1] + CP[2] + ["C.t"]
 
-    load("ldP", "A", ap("P", 0, 64), lambda T: T.pos[:], "l0", 256, ["P0"])
-    load("ldC", "S", ap("rawC", 0, L), lambda T: T.ctl[:], "l1", 2 * L, ["rawC"])
-    load("ldX", "S", ap("rawX", 0, L), lambda T: T.tape[:], "l2", 2 * L, ["rawX"])
-    load("ldCt", "A", ap("rawC", L, L + 176), lambda T: T.ctl[:, 0:176], "l3", 352, ["rawCt"])
-    load("ldXt", "A", ap("rawX", L, L + 176), lambda T: T.tape[:, 0:176], "l4", 352, ["rawXt"])
-    load("ldT", "A", ap("thi", 0, 3, p=8), lambda T: T.th[:], "l5", 12, ["thi"])
-    iota("ki", ap("ki", 0, 1), [[0, 1]], 1, 1, ["ki0"], False)
-    iota("xrow", ap("xrow", 0, 256), [[1, 256]], 0, 256, ["xrow"])
-    iota("blk", ap("blk", 0, 128), [[16, 8], [0, 16]], 0, 128, ["blk"])
-    iota("kl0", ap("kl0", 0, 10), [[16, 10]], 1, 10, ["kl0"])
+    load("ldP", "A", ap("P", 0, 64), lambda T: T.pos[:], "l0", ["P0"])
+    load("ldC", "S", ap("C", 0, L), lambda T: T.ctl[:], "l1", CT[:6])
+    load("ldX", "S", ap("rawX", 0, L), lambda T: T.tape[:], "l2", ["rawX"])
+    load("ldCt", "A", ap("C", L, WG), lambda T: T.ctl[:, 0:WG - L], "l3", ["C.t"])
+    load("ldXt", "A", ap("rawX", L, L + 176), lambda T: T.tape[:, 0:176], "l4", ["rawXt"])
+    load("ldT", "S", ap("thi", 0, 3, p=8), lambda T: T.th[:], "l5", ["thi"])
+    iota("ki", ap("ki", 0, 1), [[0, 1]], 1, ["ki0"], False)
+    iota("xrow", ap("xrow", 0, 256), [[1, 256]], 0, ["xrow"])
+    iota("blk", ap("blk", 0, 128), [[16, 8], [0, 16]], 0, ["blk"])
+    iota("kl0", ap("kl0", 0, 10), [[16, 10]], 1, ["kl0"])
     for i, mk in ((1, 0x70), (2, 0x77), (3, 8)):
-        ts("ki%d" % i, ap("ki", i, i + 1), ap("ki", 0, 1), mk, None, ALU.bitwise_and, None, 1, ["ki0"], ["ki%d" % i])
-    cp("kf", "V", ap("kf", 0, 4), ap("ki", 0, 4), 4, ["ki0", "ki1", "ki2", "ki3"], ["kf"])
-    ts("mk0", kf[4], kf[3], 0.0, 0.0625, ALU.is_equal, ALU.mult, 1, ["kf"], ["mk0"])
-    ts("mk1", kf[5], kf[3], 1.0 / 128, None, ALU.mult, None, 1, ["kf"], ["mk1"])
-    ts("pb15", kf[6], kf[1], 15.0, None, ALU.add, None, 1, ["kf"], ["pb15"])
-    ts("Z", ap("Z", 0, 144), ap("xrow", 0, 144), kf[6], 8.0, ALU.is_equal, ALU.mult, 144, ["xrow", "pb15"], ["Z"])
-    ts("ZN", ap("ZN", 0, 144), ap("xrow", 0, 144), kf[6], -8.0, ALU.is_equal, ALU.mult, 144, ["xrow", "pb15"], ["ZN"])
-    ts("ID", ap("ID", 0, 128), ap("xrow", 0, 128), kf[0], None, ALU.is_equal, None, 128, ["xrow", "kf"], ["ID"])
-    ts("NI", ap("NI", 0, 128), ap("xrow", 0, 128), kf[0], -1.0, ALU.is_equal, ALU.mult, 128, ["xrow", "kf"], ["NI"])
+        ts("ki1", ap("ki", i, i + 1), ap("ki", 0, 1), mk, None, ALU.bitwise_and, None, ["ki0"], ["ki%d" % i])
+    cp("kf", "V", ap("kf", 0, 4), ap("ki", 0, 4), ["ki0", "ki1", "ki2", "ki3"], ["kf"])
+    ts("mk", kf[4], kf[3], 0.0, 0.0625, ALU.is_equal, ALU.mult, ["kf"], ["mk0"])
+    ts("mk", kf[5], kf[3], 1.0 / 128, None, ALU.mult, None, ["kf"], ["mk1"])
+    ts("mk", kf[6], kf[1], 15.0, None, ALU.add, None, ["kf"], ["pb15"])
+    ts("Z", ap("Z", 0, 144), ap("xrow", 0, 144), kf[6], None, ALU.is_equal, None, ["xrow", "pb15"], ["Z"])
+    ts("ZN", ap("ZN", 0, 144), ap("xrow", 0, 144), kf[6], -16.0, ALU.is_equal, ALU.mult, ["xrow", "pb15"], ["ZN"])
+    ts("ID", ID, ap("xrow", 0, 128), kf[0], None, ALU.is_equal, None, ["xrow", "kf"], ["ID"])
+    ts("NI", NI, ap("xrow", 0, 128), kf[0], -16.0, ALU.is_equal, ALU.mult, ["xrow", "kf"], ["NI"])
+    ts("IF", IF, ap("xrow", 0, 128), kf[0], None, ALU.is_equal, None, ["xrow", "kf"], ["IF"])
     for r in range(8):
-        ts("B%d" % r, ap("B", 128 * r, 128 * r + 128), ap("blk", 0, 128), float(r), kf[2], ALU.add, ALU.is_equal, 128,
+        ts("B%d" % (r // 4), ap("B", 128 * r, 128 * r + 128), ap("blk", 0, 128), float(r), kf[2], ALU.add, ALU.is_equal,
            ["blk", "kf"], ["B%d" % r])
     for h in range(2):
-        ts("ZR%d" % h, ap("ZR", 128 * h, 128 * h + 128), ap("xrow", 0, 128), kf[0], 0.6, ALU.is_equal, ALU.mult, 128,
+        ts("ZR", ap("ZR", 128 * h, 128 * h + 128), ap("xrow", 0, 128), kf[0], 0.6, ALU.is_equal, ALU.mult,
            ["xrow", "kf"], ["ZR%d" % h])
-    ts("BD", ap("BD", 0, 128), ap("blk", 0, 128), kf[1], None, ALU.is_equal, None, 128, ["blk", "kf"], ["BD"])
-    ts("NU0", ap("NU0", 0, 128), ap("xrow", 0, 128), kf[0], -1.0, ALU.is_lt, ALU.mult, 128, ["xrow", "kf"], ["NU0"])
-    tt("NU", ap("NU", 0, 128), ap("NU0", 0, 128), ap("BD", 0, 128), ALU.mult, 128, ["NU0", "BD"], ["NU"])
-    ts("kl", ap("kl", 0, 10), ap("kl0", 0, 10), kf[1], None, ALU.subtract, None, 10, ["kl0", "kf"], ["kl"])
-    ts("kb", ap("kb", 0, 10), ap("kl", 0, 10), 0.5, None, ALU.add, None, 10, ["kl"], ["kb"])
-    ts("dk", ap("dk", 0, 10), ap("kl", 0, 10), 8.0, 8.0 * SP, ALU.mult, ALU.add, 10, ["kl"], ["dk"])
-    ts("E", ap("E", 0, 128, p=8), ap("blk", 0, 128, p=8), 0.0625, ap("kf", 0, 1, p=8), ALU.mult, ALU.is_equal, 128,
+    ts("BD", BD, ap("blk", 0, 128), kf[1], None, ALU.is_equal, None, ["blk", "kf"], ["BD"])
+    ts("NU0", ap("NU0", 0, 128), ap("xrow", 0, 128), kf[0], -1.0, ALU.is_lt, ALU.mult, ["xrow", "kf"], ["NU0"])
+    tt("NU", NU, ap("NU0", 0, 128), BD, ALU.mult, ["NU0", "BD"], ["NU"])
+    ts("kl", ap("kl", 0, 10), ap("kl0", 0, 10), kf[1], None, ALU.subtract, None, ["kl0", "kf"], ["kl"])
+    ts("kb", ap("kb", 0, 10), ap("kl", 0, 10), 0.5, None, ALU.add, None, ["kl"], ["kb"])
+    act("one", ap("cut", 0, 240), ap("xrow", 0, 240), ACT.Tanh, ["xrow"], ["one"], bias=16.0)
+    add("nil", "V", lambda g, T, nx: g.vector.memset(T["X"][:, WE:WG], 0.0), (), ["X.s"])
+    ts("E", ap("E", 0, 128, p=8), ap("blk", 0, 128, p=8), 0.0625, ap("kf", 0, 1, p=8), ALU.mult, ALU.is_equal,
        ["blk", "kf"], ["E"])
-    cp("thf0", "V", ap("thf0", 0, 3, p=8), ap("thi", 0, 3, p=8), 3, ["thi"], ["thf0"])
-    cp("thb", "V", ap("thb", 0, 3, p=8), ap("thf0", 0, 3, p=8), 3, ["thf0"], ["thb"])
-    ts("cvC0", ap("C", 0, 1536), ap("rawC", 0, 1536), 0.125, None, ALU.mult, None, 1536, ["rawC"], tk("C", 0, 512), kind="h")
-    ts("cvC1", ap("C", 1536, WE), ap("rawC", 1536, WE), 0.125, None, ALU.mult, None, WE - 1536, ["rawC", "rawCt"],
-       tk("C", 512, K) + ["C.t"], kind="h")
+    cp("th0", "V", ap("thf0", 0, 3, p=8), ap("thi", 0, 3, p=8), ["thi"], ["thf0"])
+    cp("th1", "V", ap("thb", 0, 3, p=8), ap("thf0", 0, 3, p=8), ["thf0"], ["thb"])
+    mm("th2", [(ps(SR + 240, 3), ap("E", 0, 128, p=8), ap("thb", 0, 3, p=8), True, True)], ["E", "thb"], ["th"], [7])
+    ts("th3", ap("thf", 0, 3), ps(SR + 240, 3), -QS, None, ALU.add, None, ["th"], ["thf"], [7])
     for j in (1, 2):
-        add("cvX%d" % j, "G", lambda g, T, nx, j=j: g.affine_select(T["X"][:, j:WE:3], T["rawX"][:, j:WE:3], [[0, WE // 3]],
-                                                                  ALU.is_ge, 0.0, 0, 0),
-            ("g", WE // 3), ["rawX", "rawXt"], ["X.%d" % j])
-    if max(cfg["upe"]) or max(cfg["fold"]):
-        ts("IF", ap("IF", 0, 128), ap("xrow", 0, 128), kf[0], None, ALU.is_equal, None, 128, ["xrow", "kf"], ["IF"])
+        cp("cv%d.0" % j, "G", ap("X", j, WE, 3), ap("rawX", j, WE, 3), ["rawX", "rawXt"], ["X.p%d" % j], n=WE // 3)
 
     def lists(t):
         c0 = 64 * t
-        src, off, rd = ap("P", c0, c0 + 64), 8.0 * t - 0.46875, ["P%d" % t]
-        ts("v%d" % t, ap("v16", c0, c0 + 64), src, 0.0625, off, ALU.mult, ALU.add, 64, rd, ["v%d" % t])
-        ts("w%d" % t, ap("w16", c0, c0 + 64), src, 0.0625, off + 1.0, ALU.mult, ALU.add, 64, rd, ["w%d" % t])
-        ts("lo%d" % t, ap("lo", c0, c0 + 64), src, 15, None, ALU.bitwise_and, None, 64, rd, ["lo%d" % t])
+        src, off, rd = ap("P", c0, c0 + 64), QS / 16 * max(t - 1, 0) - 0.46875, ["P%d" % t]
+        ts("v.%d" % t, ap("v16", c0, c0 + 64), src, 0.0625, off, ALU.mult, ALU.add, rd, ["v%d" % t])
+        ts("w.%d" % t, ap("w16", c0, c0 + 64), src, 0.0625, off + 1.0, ALU.mult, ALU.add, rd, ["w%d" % t])
+        ts("w.%d" % t, ap("lo", c0, c0 + 64), src, 15, None, ALU.bitwise_and, None, rd, ["lo%d" % t])
         for h in range(2):
-            ts("f%d_%d" % (t, h), ap("ph", 128 * t + h, 128 * t + 128, 2), ap("lo", c0, c0 + 64), kf[4 + h], None, ALU.mult, None,
-               64, ["lo%d" % t, "mk%d" % h], ["ph%d_%d" % (t, h)])
+            ts("f.%d" % t, ap("ph", 128 * t + h, 128 * t + 128, 2), ap("lo", c0, c0 + 64), kf[4 + h], None, ALU.mult, None,
+               ["lo%d" % t, "mk%d" % h], ["ph%d_%d" % (t, h)])
+
+    def floor16(name, out, in_, r, w):
+        if name in cfg["qa"]:
+            act(name, out, in_, ACT.Identity, r, w, bias=QB - 0.46875, scale=0.0625)
+        else:
+            ts(name, out, in_, 0.0625, QB - 0.46875, ALU.mult, ALU.add, r, w)
+
+    def plane_sums(t, dst, tok):
+        j, o, qn = t % 3, K * (t % 2), "qn%d" % (t % 2)
+        for h in range(2):
+            floor16("r%d.%d" % (h, t), ap("qn", o + 512 * h, o + 512 * h + 512), ap("C", 1536 * h + j, 1536 * h + 1536, 3),
+                    [CP[j][h]], tk(qn, 512 * h, 512 * h + 512))
+        if t < RO - 3:
+            x, q = [ap("C", 3 * r + j, L, 48) for r in range(16)], [ap("qn", o + r, o + K, 16) for r in range(16)]
+        else:
+            x = [ap("C", 192 * r + j, 192 * r + 192, 3) for r in range(16)]
+            q = [ap("qn", o + 64 * r, o + 64 * r + 64) for r in range(16)]
+        mm("Sn.%d" % t, [(dst, Wr[r], x[r], r == 0, False) for r in range(16)], ["Z"] + CP[j], [tok], [7], "o")
+        mm("Sq.%d" % t, [(dst, Wn[r], q[r], False, r == 15) for r in range(16)], ["ZN"] + tk(qn, 0, K), [tok], [7], "c")
 
     def control(t):
         j, o = t % 3, K * (t % 2)
-        cb, sg = "cb%d" % (t % 2), "sg%d" % (t % 2)
-        win, rd, sc = ("rawC", ["rawC", "rawCt"], 0.125) if t == 0 else ("C", CT, 1.0)
+        xb, qb = "xb%d" % (t % 2), "qb%d" % (t % 2)
+        red = t in cfg["red"]
         for h in range(2):
             h0, h1 = 512 * h, 512 * h + 512
-            gi = ind(win, 0, WE, "v16", 64 * t + h0 // 16, 64 * t + h1 // 16)
-            if str(h) in cfg["cgv"][t]:
-                ts("c%d_%d" % (t, h), ap("cb", o + h0, o + h1), gi, sc, -1.0, ALU.mult, ALU.add, 512, rd + ["v%d" % t],
-                   tk(cb, h0, h1), kind="i")
-            else:
-                act("c%d_%d" % (t, h), ap("cb", o + h0, o + h1), gi, ACT.Identity, 512, rd + ["v%d" % t], tk(cb, h0, h1),
-                    kind="i", bias=-1.0, scale=sc)
-        sp = cfg["split"][t]
-        for h in range(2):
-            h0, h1 = 512 * h, 512 * h + 512
-            mm("to%d_%d" % (t, h), [(ap("TP", h0, h1), ap("ID", 0, 128), ap("C", 3 * h0 + j, 3 * h1, 3), True, False, 512)],
-               ["ID"] + tk("C", h0, h1), ["TP%d" % h], ["TP%d" % h])
-            mm("t%d_%d" % (t, h), [(ap("TP", h0, h1), ap("ID", 0, 128), ap("cb", o + h0, o + h1), False, True, 512)],
-               ["ID"] + tk(cb, h0, h1), ["TP%d" % h], ["TP%d" % h])
-            if h0 < sp:
-                mm("uo%d" % t, [(ap("T2", 0, 512), ap("ID", 0, 128), ap("C", j, 1536, 3), True, False, 512)],
-                   ["ID"] + tk("C", h0, h1), ["T2"], ["T2"])
-                mm("ut%d" % t, [(ap("T2", 0, 512), ap("ID", 0, 128), ap("cb", o, o + 512), False, False, 512)],
-                   ["ID"] + tk(cb, h0, h1), ["T2"], ["T2"])
-            act("sg%d_%d" % (t, h), ap("sg", o + h0, o + h1), ap("TP", h0, h1), ACT.Sign, 512, ["TP%d" % h], tk(sg, h0, h1),
-                ["TP%d" % h], bias=-0.9375)
-        mm("cs%d" % t, [(ap("SM", 0, 64), Wr[r], ap("cb", o + r, o + K, 16), r == 0, r == 15, 64) for r in range(16)],
-           ["Z"] + tk(cb, 0, K), ["SM"], ["SM"])
-        tt("p%d" % t, ap("P", 64 * t + 64, 64 * t + 128), ap("SM", 0, 64), ap("P", 64 * t, 64 * t + 64), ALU.add, 64,
-           ["SM", "P%d" % t], ["P%d" % (t + 1)], ["SM"])
+            cp("x%d.%d" % (h, t), "V" if str(h) in cfg["xv"][t] else "A", ap("xb", o + h0, o + h1),
+               ind("C", 0, WE if t else L, "v16", 64 * t + h0 // 16, 64 * t + h1 // 16), CT[:7 if t else 6] + ["v%d" % t], tk(xb, h0, h1))
+            if t > 0:
+                floor16("q%d.%d" % (h, t), ap("qb", o + h0, o + h1), ap("xb", o + h0, o + h1), tk(xb, h0, h1), tk(qb, h0, h1))
+        mm("cx.%d" % t, [(ps(SM, 64), Wr[r], ap("xb", o + r, o + K, 16), r == 0, t == 0 and r == 15) for r in range(16)],
+           ["Z"] + tk(xb, 0, K), ["SM"], [7], "o" if t else "oc")
+        if t > 0:
+            mm("cq.%d" % t, [(ps(SM, 64), Wn[r], ap("qb", o + r, o + K, 16), False, r == 15) for r in range(16)],
+               ["ZN"] + tk(qb, 0, K), ["SM"], [7], "c")
+        tt("p.%d" % t, ap("P", 64 * t + 64, 64 * t + 128), ps(SM, 64), ap("P", 64 * t, 64 * t + 64), ALU.add,
+           ["SM", "P%d" % t], ["P%d" % (t + 1)], [7])
         if t < RO - 1:
             lists(t + 1)
-        if j == 2 and t < RO - 1:
-            mm("So%d" % t, [(ap("SM", 64, 128), Wr[r], ap("C", 3 * r + 2, L, 48), r == 0, False, 64) for r in range(16)]
-               + [(ap("SM", 64, 128), Wr[r], ap("cb", o + r, o + K, 16), False, False, 64) for r in range(16)],
-               ["Z"] + tk("C", 0, K) + tk(cb, 0, K), ["SM1"], ["SM"])
-            mm("S%d" % t, [(ap("SM", 64, 128), ap("ZN", 15 - r, 143 - r), ap("sg", o + r, o + K, 16), False, r == 15, 64)
-                           for r in range(16)], ["ZN"] + tk(sg, 0, K), ["SM1"], ["SM"])
+        bias = 16 * QB if red else 0.0
         for h in range(2):
-            h0, h1 = 512 * h, 512 * h + 512
-            if h0 < sp:
-                src, bk = "T2", "T2"
-                mm("ac%d" % t, [(ap("T2", 0, 512), ap("NI", 0, 128), ap("sg", o, o + 512), False, True, 512)],
-                   ["NI"] + tk(sg, h0, h1), [bk], [bk])
-                cp("cn%d_%d" % (t, h), "A", ap("C", 3 * h0 + j, 3 * h1, 3), ap(src, h0, h1), 512, [bk], tk("C", h0, h1), [bk])
-                if h == 0 and t < RO - 1:
-                    cp("ct%d" % t, "A", ap("C", L + j, WE, 3), ap(src, 0, TL // 3), TL // 3, [bk], ["C.t"], [bk])
+            h0, h1, tp = 512 * h, 512 * h + 512, "TP%d" % h
+            old, dst = ap("C", 3 * h0 + j, 3 * h1, 3), ps(TP + h0, 512)
+            mm("to%d.%d" % (h, t), [(dst, ID, old, True, False)], ["ID", CP[j][h]], [tp], [4 + h], "o")
+            mm("tx%d.%d" % (h, t), [(dst, ID, ap("xb", o + h0, o + h1), False, not red)]
+               + ([(dst, NI, ap("qb", o + h0, o + h1), False, True)] if red else []),
+               ["ID", "NI"] + tk(xb, h0, h1) + (tk(qb, h0, h1) if red else []), [tp], [4 + h], "c")
+        for h in range(2):
+            h0, h1, tp = 512 * h, 512 * h + 512, "TP%d" % h
+            name, new = "cn%d.%d" % (h, t), ap("C", 3 * h0 + j, 3 * h1, 3)
+            if str(h) in cfg["cv"][t]:
+                ts(name, new, ps(TP + h0, 512), bias, None, ALU.add, None, [tp], [CP[j][h]], [4 + h])
             else:
-                bk = "TP%d" % h
-                tt("cn%d_%d" % (t, h), ap("C", 3 * h0 + j, 3 * h1, 3), ap("TP", h0, h1), ap("sg", o + h0, o + h1), ALU.subtract,
-                   512, [bk] + tk(sg, h0, h1), tk("C", h0, h1), [bk])
-                if h == 0 and t < RO - 1:
-                    tt("ct%d" % t, ap("C", L + j, WE, 3), ap("TP", 0, TL // 3), ap("sg", o, o + TL // 3), ALU.subtract,
-                       TL // 3, [bk] + tk(sg, 0, 128), ["C.t"], [bk])
+                act(name, new, ps(TP + h0, 512), ACT.Identity, [tp], [CP[j][h]], [4 + h], bias=bias)
+            if h == 0 and t < RO - 1 and j != 2:
+                if cfg["ct"] == "G":
+                    cp("ct.%d" % t, "G", ap("C", L + j, WE, 3), ap("C", j, TL, 3), [CP[j][0]], ["C.t"], n=TL // 3)
+                else:
+                    act(name, ap("C", L + j, WE, 3), ps(TP, TL // 3), ACT.Identity, [tp], ["C.t"], [4], bias=bias)
+        if t >= RO - 3:
+            plane_sums(t, ps(SR + j, 192 - j, 3), "yc")
 
-    def razor_control(m):
-        c64, c16, c32 = 64 * m, 16 * m, 32 * m
-        n = lambda s: "%s%d" % (s, m)
-        ts(n("cut"), ap("cut", c64, c64 + 64), ap("SM", 64, 128), ap("thf", m, m + 1), None, ALU.is_ge, None, 64,
-           ["SM1", "thf"], [n("cut")], ["SM"])
-        add(n("inc"), "V", lambda g, T, nx: g.vector.tensor_tensor_scan(T["inc"][:, c64:c64 + 64], T["cut"][:, c64:c64 + 64],
-                                                                       T["cut"][:, c64:c64 + 64], 0.0, ALU.add, ALU.max),
-            ("v", 64), [n("cut")], [n("inc")])
-        mm(n("M"), [(ap("SM", 192, 256), ap("BD", 0, 128), ap("inc", c64, c64 + 64), True, True, 64),
-                    (ap("SM", 128, 192), ap("BD", 0, 128), ap("inc", c64, c64 + 64), True, False, 64),
-                    (ap("SM", 128, 192), ap("NU", 0, 128), ap("cut", c64, c64 + 64), False, True, 64)],
-           ["BD", "NU", n("inc"), n("cut")], ["SM2"], ["SM"])
-        c128 = 128 * m
+    def razor_control(t):
+        m = t // 3
+        c80, c16, c32, c96 = 80 * m, 16 * m, 32 * m, 96 * m
+        n = lambda s: "%s.%d" % (s, t)
+        plane_sums(t, ps(SR, 64), "S")
+        cut, inc, cum, pre, ids = ap("cut", c80, c80 + NB), ap("inc", c80, c80 + NB), ps(SR + 64, NB), ps(SR + 64 + NB, NB), ps(SR + 224, 10)
+        ts(n("cut"), ap("cut", c80, c80 + 64), ps(SR, 64), ap("thf", m, m + 1), None, ALU.is_ge, None, ["S", "thf", "one"], [n("cut")], [7])
+        add(n("inc"), "V", lambda g, T, nx: g.vector.tensor_tensor_scan(inc(T), cut(T), cut(T), 0.0, ALU.add, ALU.max),
+            [n("cut")], [n("inc")])
+        mm(n("M"), [(cum, BD, inc, True, True), (pre, BD, inc, True, False), (pre, NU, cut, False, True)],
+           ["BD", "NU", n("inc"), n("cut")], ["M"], [7])
         for kk in range(10):
-            add("J%d_%d" % (m, kk), "A", lambda g, T, nx, kk=kk: g.scalar.activation(
-                T["junk"][:, 64 * kk:64 * kk + 64], T["SM"][:, 192:256], ACT.Sign,
+            add(n("J%d" % (kk // 5)), "A", lambda g, T, nx, kk=kk: g.scalar.activation(
+                T["junk"][:, 80 * kk:80 * kk + NB], cum(T), ACT.Sign,
                 bias=T["kb"][:, kk:kk + 1], scale=-1.0, accum_out=T["JS"][:, c16 + kk:c16 + kk + 1]),
-                ("v", 84), ["SM2", "kb"], ["JS%d_%d" % (m, kk), "junk%d" % kk], ["SM"])
-        cp(n("MS"), "A", ap("MS", c128, c128 + 128), ap("SM", 128, 256), 128, ["SM2"], [n("MS")], ["SM"])
-        send(n("sn"), ap("nb", 4 * m, 4 * m + 4), ap("MS", c128 + 124, c128 + 128), n("rn"), 16, [n("MS")], [n("nb")])
-        js = ["JS%d_%d" % (m, kk) for kk in range(10)]
-        ts(n("J16"), ap("J16", c16, c16 + 10), ap("JS", c16, c16 + 10), 0.5, 32.0, ALU.mult, ALU.add, 10, js, [n("J16")])
-        act(n("Jb"), ap("Jb", c16, c16 + 10), ap("JS", c16, c16 + 10), ACT.Identity, 10, js, [n("Jb")], bias=4096.0, scale=64.0)
-        tt(n("cmp"), ap("cmp", 160 * m, 160 * m + 160), ind("MS", c128, c128 + 128, "J16", c16, c16 + 10), ap("xrow", 0, 160),
-           ALU.is_le, 160, [n("MS"), n("J16"), "xrow"], [n("cmp")], kind="i")
-        mm(n("R"), [(ap("SM", 256, 266), ap("ID", 0, 128), ap("Jb", c16, c16 + 10), True, False, 64)]
-           + [(ap("SM", 256, 266), Wr[r], ap("cmp", 160 * m + r, 160 * m + 160, 16), False, r == 15, 64) for r in range(16)],
-           ["Z", "ID", n("Jb"), n("cmp")], ["SM3"], ["SM"])
+                ["M", "kb"], [n("JS%d" % kk), "junk%d" % kk], [7])
+        cp(n("MS"), cfg["ms"], ap("MS", c96, c96 + NB + 16), ps(SR + 124, NB + 16), ["M"], [n("MS")], [7])
+        send(n("sn"), ap("nb", 4 * m, 4 * m + 4), ap("MS", c96, c96 + 4), "rn%d" % m, [n("MS")], [n("nb")])
+        js = [n("JS%d" % kk) for kk in range(10)]
+        ts(n("J16"), ap("J16", c16, c16 + 10), ap("JS", c16, c16 + 10), 0.5, NB / 2, ALU.mult, ALU.add, js, [n("J16")])
+        act(n("Jb"), ap("Jb", c16, c16 + 10), ap("JS", c16, c16 + 10), ACT.Identity, js, [n("Jb")], bias=8.0 * NB, scale=8.0)
+        tt(n("cmp"), ap("cmp", 160 * m, 160 * m + 160), ind("MS", c96 + 16, c96 + 16 + NB, "J16", c16, c16 + 10), ap("xrow", 0, 160),
+           ALU.is_le, [n("MS"), n("J16"), "xrow"], [n("cmp")])
+        mm(n("R"), [(ids, ID, ap("Jb", c16, c16 + 10), True, False)]
+           + [(ids, Wr[r], ap("cmp", 160 * m + r, 160 * m + 160, 16), False, r == 15) for r in range(16)],
+           ["Z", "ID", n("Jb"), n("cmp")], ["R"], [7])
         for c in range(3):
-            ts("gl%d_%d" % (m, c), ap("gl", c32 + 10 * c, c32 + 10 * c + 10), ap("SM", 256, 266), 0.375, float(c), ALU.mult, ALU.add,
-               10, ["SM3"], ["gl%d_%d" % (m, c)], ["SM"])
-        cp(n("id8"), "A", ap("id8", c16, c16 + 10), ap("SM", 256, 266), 10, ["SM3"], [n("id8")], ["SM"])
-        gl = ["gl%d_%d" % (m, c) for c in range(3)]
-        cp(n("gC"), cfg["gc"], ap("mC", 480 * m, 480 * m + 480), ind("C", 0, WE, "gl", c32, c32 + 30), 480, CT + gl, [n("mC")], kind="i")
-        send(n("sC"), ap("lC", 480 * m, 480 * m + 480), ap("mC", 480 * m, 480 * m + 480), n("rc"), 960, [n("mC")], [n("lC")])
-        ts(n("gid"), ap("gid", c16, c16 + 10), ap("id8", c16, c16 + 10), 0.125, float(K - 1), ALU.mult, ALU.min, 10, [n("id8")], [n("gid")])
-        tt(n("nm"), ap("nm", m, m + 1), ap("nb", 4 * m + 3, 4 * m + 4), ap("MS", c128 + 127, c128 + 128), ALU.min, 1,
-           [n("nb"), n("MS")], [n("nm")])
-        ts(n("iv"), ap("iv", c16, c16 + 10), ap("kl", 0, 10), ap("nm", m, m + 1), None, ALU.is_ge, None, 10, ["kl", n("nm")], [n("iv")])
-        tt(n("dkv"), ap("dkv", c16, c16 + 10), ap("iv", c16, c16 + 10), ap("dk", 0, 10), ALU.mult, 10, ["dk", n("iv")], [n("dkv")])
-        tt(n("y8"), ap("y8", c16, c16 + 10), ap("id8", c16, c16 + 10), ap("dkv", c16, c16 + 10), ALU.max, 10,
-           [n("id8"), n("dkv")], [n("y8")])
+            ts(n("gl"), ap("gl", c32 + 10 * c, c32 + 10 * c + 10), ids, 3.0, float(c), ALU.mult, ALU.add, ["R"], [n("gl%d" % c)], [7])
+        if "P" not in cfg["sp"][cfg["steps"][t]]["ue"]:
+            ts(n("gid"), ap("gid", c16, c16 + 10), ids, float(K - 1), None, ALU.min, None, ["R"], [n("gid")], [7])
+        ts(n("iv"), ap("iv", c16, c16 + 10), ap("kl", 0, 10), ap("nb", 4 * m + 3, 4 * m + 4), float(SP), ALU.is_ge, ALU.mult,
+           ["kl", n("nb")], [n("iv")])
+        tt(n("y"), ap("y", c16, c16 + 10), ids, ap("iv", c16, c16 + 10), ALU.add, ["R", n("iv")], [n("y")], [7])
         for c in range(3):
-            ts("sl%d_%d" % (m, c), ap("sl", c32 + 10 * c, c32 + 10 * c + 10), ap("y8", c16, c16 + 10), 0.375, float(c), ALU.mult, ALU.add,
-               10, [n("y8")], ["sl%d_%d" % (m, c)])
-        cp(n("xC"), "V", ind("C", 0, WW, "sl", c32, c32 + 30), ap("lC", 480 * m, 480 * m + 480), 480,
-           [n("lC")] + ["sl%d_%d" % (m, c) for c in range(3)], CT, kind="x")
-        cp(n("xCt"), "A", ap("C", L, WE), ap("C", 0, TL), TL, tk("C", 0, 128), ["C.t"])
+            ts(n("sl"), ap("sl", c32 + 10 * c, c32 + 10 * c + 10), ap("y", c16, c16 + 10), 3.0, float(c), ALU.mult, ALU.add,
+               [n("y")], [n("sl%d" % c)])
+        gl, sl = [n("gl%d" % c) for c in range(3)], [n("sl%d" % c) for c in range(3)]
+        for x, l0, l1 in cfg["sc"]:
+            e0, e1 = 480 * m + 16 * l0, 480 * m + 16 * l1
+            cp(n("g" + x), "A", ap("mC", e0, e1), ind("C", 0, WG, "gl", c32 + l0, c32 + l1), CT + gl, [n("m" + x)])
+            send(n("s" + x), ap("lC", e0, e1), ap("mC", e0, e1), "r%s%d" % (x.lower(), m), [n("m" + x)], [n("l" + x)])
+        for x, l0, l1 in cfg["sc"]:
+            e0, e1 = 480 * m + 16 * l0, 480 * m + 16 * l1
+            cp(n("x" + x), "V", ind("C", 0, WW, "sl", c32 + l0, c32 + l1), ap("lC", e0, e1), [n("l" + x)] + sl, CT)
+        cp(n("xCt"), cfg["xct"], ap("C", L, WE), ap("C", 0, TL), [CP[0][0], CP[1][0], CP[2][0]], ["C.t"], n=TL)
 
     def signal(t):
-        j, o, so = t % 3, K * (t % 2), K * t
-        m = t // 3
-        raz = j == 2 and t < RO - 1
-        a, u, s = "a%d" % t, "u%d" % (t % 2), "s%d" % t
+        j, o, so, m = t % 3, K * (t % 2), K * t, t // 3
+        raz, end = j == 2 and t < RO - 1, t == RO - 1
+        n = lambda s: "%s.%d" % (s, t)
+        a, u, s = "a%d" % (t % 2), "u%d" % (t % 2), "s%d" % t
         win, rd = ("rawX", ["rawX", "rawXt"]) if t == 0 else ("X", XT)
         for b in range(2):
-            mm("ph%d_%d" % (t, b), [(ap("PH", 512 * b + r, 512 * b + 512, 8), ap("B", 128 * r, 128 * r + 128),
-                                     ap("ph", 128 * t + 64 * b, 128 * t + 64 * b + 64), True, True, 64) for r in range(8)],
-               ["B%d" % r for r in range(8)] + ["ph%d_0" % t, "ph%d_1" % t], tk("PH", 512 * b, 512 * b + 512), ["PH%d" % b])
-        ms, upe = cfg["ms"], cfg["upe"][t]
-        fold = cfg["fold"][t]
-        ad = cfg["ad"]
+            mm(n("ph%d" % b), [(ps(PH + 512 * b + r, 512 - r, 8), ap("B", 128 * r, 128 * r + 128),
+                                ap("ph", 128 * t + 64 * b, 128 * t + 64 * b + 64), True, True) for r in range(8)],
+               ["B%d" % r for r in range(8)] + ["ph%d_0" % t, "ph%d_1" % t], tk("PH", 512 * b, 512 * b + 512), [b])
+        sp = cfg["sp"][cfg["steps"][t]]
+        ad, uc, ue = sp["ad"], sp["uc"], sp["ue"] if t else "VVVV"
+        slot = cfg["slot"][t]
+        a, ao = "a%d" % slot, K * slot
         for k in range(len(ad) - 1):
             h0, h1 = ad[k], ad[k + 1]
             l0, l1 = 64 * t + h0 // 16, 64 * t + h1 // 16
-            cp("a%d_%d" % (t, k), "A", ap("a", so + h0, so + h1), ind(win, 0, WE, "v16", l0, l1), h1 - h0, rd + ["v%d" % t],
-               tk(a, h0, h1), kind="i")
-            tt("d%d_%d" % (t, k), ap("s", so + h0, so + h1), ind(win, 0, WE, "w16", l0, l1), ap("a", so + h0, so + h1), ALU.subtract,
-               h1 - h0, rd + ["w%d" % t] + tk(a, h0, h1), tk(s, h0, h1), kind="i")
+            cp(n("a%d" % k), "A", ap("a", ao + h0, ao + h1), ind(win, 0, WE if t else L, "v16", l0, l1), rd[:None if t else 1] + ["v%d" % t], tk(a, h0, h1))
+            tt(n("d%d" % k), ap("s", so + h0, so + h1), ind(win, 0, WE, "w16", l0, l1), ap("a", ao + h0, ao + h1), ALU.subtract,
+               rd + ["w%d" % t] + tk(a, h0, h1), tk(s, h0, h1))
+        banks = list(zip(sp["zb"], (2, 3, 6)))
+        zb = lambda h: max(e for e in banks if e[0] <= h)
+        zp = lambda h0, h1: ps(512 * zb(h0)[1] + h0 - zb(h0)[0], h1 - h0)
+        kind = lambda h: ue[max(k for k in range(len(uc) - 1) if uc[k] <= h)]
         if t > 0:
             sh = 16 * (t % 8)
-            for k in range(2):
-                h0, h1 = ms[k], ms[k + 1]
-                fo = str(k) in fold
-                if fo:
-                    mm("ia%d_%d" % (t, k), [(ap("ZP", h0, h1), ap("IF", 0, 128), ap("a", so + h0, so + h1), True, False, 4 * (h1 - h0))],
-                       ["IF"] + tk(a, h0, h1), tk("ZP", h0, h1), ["ZP%d" % k])
-                mm("ro%d_%d" % (t, k), [(ap("ZP", h0, h1), ap("ZR", sh, sh + 128), ap("z", so - K + h0, so - K + h1), not fo, h0 >= upe,
-                                         4 * (h1 - h0))],
-                   ["ZR0", "ZR1", "z%d_%d" % (t - 1, k)], tk("ZP", h0, h1), ["ZP%d" % k])
+            for b, (h0, bk) in enumerate(banks):
+                h1, x = (banks + [(K, 0)])[b + 1][0], kind(h0)
+                if x == "F":
+                    mm(n("ia%d" % b), [(zp(h0, h1), IF, ap("a", ao + h0, ao + h1), True, False)],
+                       ["IF"] + tk(a, h0, h1), tk("ZP", h0, h1), [bk], "o")
+                mm(n("ro%d" % b), [(zp(h0, h1), ap("ZR", sh, sh + 128), ap("z", so - K + h0, so - K + h1), x != "F", x != "P")],
+                   ["ZR0", "ZR1"] + tk("z%d" % (t - 1), h0, h1), tk("ZP", h0, h1), [bk], {"P": "o", "V": "oc", "F": "c"}[x])
         if raz:
-            cp("gX%d" % m, cfg["gx"], ap("mX", 480 * m, 480 * m + 320), ind("X", 0, WE, "gl", 32 * m, 32 * m + 20), 320,
-               XT + ["gl%d_0" % m, "gl%d_1" % m], ["mX%d" % m], kind="i")
-            send("sX%d" % m, ap("lX", 480 * m, 480 * m + 320), ap("mX", 480 * m, 480 * m + 320), "rx%d" % m, 1280,
-                 ["mX%d" % m], ["lX%d" % m])
-        if t == RO - 1:
-            ms = cfg["last"]
+            cp(n("gX"), "A", ap("mX", 480 * m, 480 * m + 320), ind("X", 0, WG, "gl", 32 * m, 32 * m + 20),
+               XT + [n("gl0"), n("gl1")], [n("mX")])
+            send(n("sX"), ap("lX", 480 * m, 480 * m + 320), ap("mX", 480 * m, 480 * m + 320), "rx%d" % m, [n("mX")], [n("lX")])
+        ms, sz = sp["ms"], sp["sz"]
         for k in range(len(ms) - 1):
             h0, h1 = ms[k], ms[k + 1]
-            bk = ["PH%d" % (h0 // 512)]
-            if str(h0 // 512) in fold:
-                tt("m%d_%d" % (t, k), ap("s", so + h0, so + h1), ap("s", so + h0, so + h1), ap("PH", h0, h1), ALU.mult, h1 - h0,
-                   tk(s, h0, h1) + tk("PH", h0, h1), tk(s, h0, h1), bk)
-                if t < RO - 1:
-                    send("sz%d_%d" % (t, k), ap("z", so + h0, so + h1), ap("s", so + h0, so + h1), "z%d_%d" % (t, k), 4 * (h1 - h0),
-                         tk(s, h0, h1) + tk(a, h0, h1), ["z%d_%d" % (t, k)], ap("a", so + h0, so + h1))
+            f, sk, bk = ps(PH + h0, h1 - h0), ap("s", so + h0, so + h1), sorted({h0 // 512, (h1 - 1) // 512})
+            if kind(h0) == "F":
+                tt(n("m%d" % k), sk, sk, f, ALU.mult, tk(s, h0, h1) + tk("PH", h0, h1), tk(s, h0, h1), bk)
                 continue
-            tt("m%d_%d" % (t, k), ap("PH", h0, h1), ap("s", so + h0, so + h1), ap("PH", h0, h1), ALU.mult, h1 - h0,
-               tk(s, h0, h1) + tk("PH", h0, h1), tk("PH", h0, h1), bk)
-            tt("s%d_%d" % (t, k), ap("s", so + h0, so + h1), ap("PH", h0, h1), ap("a", so + h0, so + h1), ALU.add, h1 - h0,
-               tk(a, h0, h1) + tk("PH", h0, h1), tk(s, h0, h1), bk)
-            if t < RO - 1:
-                send("sz%d_%d" % (t, k), ap("z", so + h0, so + h1), ap("s", so + h0, so + h1), "z%d_%d" % (t, k), 4 * (h1 - h0),
-                     tk(s, h0, h1), ["z%d_%d" % (t, k)])
-        uc = cfg["last"] if t == RO - 1 else cfg["u"]
+            tt(n("m%d" % k), f, sk, f, ALU.mult, tk(s, h0, h1) + tk("PH", h0, h1), tk("PH", h0, h1), bk)
+            tt(n("s%d" % k), sk, f, ap("a", ao + h0, ao + h1), ALU.add, tk(a, h0, h1) + tk("PH", h0, h1), tk(s, h0, h1), bk)
+        for k in range(len(sz) - 1):
+            h0, h1 = sz[k], sz[k + 1]
+            fo = kind(h0) == "F"
+            send(n("sz%d" % k), ap("z", so + h0, so + h1), ap("s", so + h0, so + h1), "z%d_%d" % (t, k),
+                 tk(s, h0, h1) + (tk(a, h0, h1) if fo else []), tk("z%d" % t, h0, h1), ap("a", ao + h0, ao + h1) if fo else None)
         src, sof, st = ("s", so, s) if t == 0 else ("u", o, u)
-        if t > 0:
-            for k in range(len(uc) - 1):
-                h0, h1 = uc[k], uc[k + 1]
-                if h0 < upe:
-                    if h0 % 512 == 0:
-                        mm("u%d_%d" % (t, k), [(ap("ZP", h0, h0 + 512), ap("IF", 0, 128), ap("s", so + h0, so + h0 + 512),
-                                                False, True, 2048)],
-                           ["IF"] + tk(s, h0, h0 + 512), tk("ZP", h0, h0 + 512), ["ZP%d" % (h0 // 512)])
-                    continue
-                tt("u%d_%d" % (t, k), ap("u", o + h0, o + h1), ap("ZP", h0, h1), ap("s", so + h0, so + h1), ALU.add, h1 - h0,
-                   tk(s, h0, h1) + tk("ZP", h0, h1), tk(u, h0, h1), ["ZP%d" % (h0 // 512)])
-        c0 = 480 * m + 320
-        if raz and not upe:
-            if cfg["x2"] == "V":
-                act("gY%d" % m, ap("mX", c0, c0 + 160), ind("u", o, o + K, "gid", 16 * m, 16 * m + 10), ACT.Tanh, 160,
-                    tk(u, 0, K) + ["gid%d" % m], ["mY%d" % m], kind="i", scale=0.625)
+        for k in range(len(uc) - 1 if t else 0):
+            h0, h1 = uc[k], uc[k + 1]
+            if ue[k] != "P":
+                tt(n("u%d" % k), ap("u", o + h0, o + h1), zp(h0, h1), ap("s", so + h0, so + h1), ALU.add,
+                   tk(s, h0, h1) + tk("ZP", h0, h1), tk(u, h0, h1), [zb(h0)[1]])
             else:
-                act("gY%d" % m, ap("mX", c0, c0 + 160), ind("u", o, o + K, "gid", 16 * m, 16 * m + 10), ACT.Identity, 160,
-                    tk(u, 0, K) + ["gid%d" % m], ["mY%d" % m], kind="i", scale=0.625)
-            send("sY%d" % m, ap("lX", c0, c0 + 160), ap("mX", c0, c0 + 160), "ry%d" % m, 640, ["mY%d" % m], ["lY%d" % m])
+                mm(n("u%d" % k), [(zp(h0, h1), IF, ap("s", so + h0, so + h1), False, True)],
+                   ["IF"] + tk(s, h0, h1), tk("ZP", h0, h1), [zb(h0)[1]], "c")
+        c0 = 480 * m + 320
+        if raz and "P" not in ue:
+            act(n("gY"), ap("mX", c0, c0 + 160), ind("u", o, o + K, "gid", 16 * m, 16 * m + 10), ACT.Tanh if cfg["xy"] == "V" else ACT.Identity,
+                tk(u, 0, K) + [n("gid")], [n("mY")], scale=0.625)
         for k in range(len(uc) - 1):
             h0, h1 = uc[k], uc[k + 1]
-            q, qo, qt, bk = ("ZP", 0, "ZP", ["ZP%d" % (h0 // 512)]) if h0 < upe else (src, sof, st, [])
-            act("x%d_%d" % (t, k), ap("X", 3 * h0 + j, 3 * h1, 3), ap(q, qo + h0, qo + h1), ACT.Tanh, h1 - h0,
-                tk(qt, h0, h1), tk("X", h0, h1), bk, scale=0.625)
-            if k == 0 and t < RO - 1 and not raz:
-                act("xt%d" % t, ap("X", L + j, WE, 3), ap(q, qo, qo + TL // 3), ACT.Tanh, TL // 3, tk(qt, 0, 128), ["X.t"], bk,
-                    scale=0.625)
-            if t == RO - 1:
-                store("stX%d" % k, lambda T, h0=h0, h1=h1: T.yx[:, 3 * h0:3 * h1], ap("X", 3 * h0, 3 * h1), 12 * (h1 - h0),
-                      tk("X", h0, h1))
-        if raz and upe:
-            cp("gY%d" % m, "A", ap("mX", c0, c0 + 160), ind("X", 0, WE, "gl", 32 * m + 20, 32 * m + 30), 160,
-               XT + ["gl%d_2" % m], ["mY%d" % m], kind="i")
-            send("sY%d" % m, ap("lX", c0, c0 + 160), ap("mX", c0, c0 + 160), "ry%d" % m, 640, ["mY%d" % m], ["lY%d" % m])
+            pe = t > 0 and ue[k] == "P"
+            q = zp if pe else (lambda x0, x1: ap(src, sof + x0, sof + x1))
+            qt, bk = ("ZP", [zb(h0)[1]]) if pe else (st, [])
+            if end:
+                act(n("t%d" % k), ap("Y", 3 * h0 + j, 3 * h1, 3), q(h0, h1), ACT.Tanh, tk(qt, h0, h1), tk("Y", h0, h1), bk, scale=0.625)
+                store(n("st%d" % k), lambda T, h0=h0, h1=h1: T.yx[:, 3 * h0:3 * h1], ap("Y", 3 * h0, 3 * h1),
+                      tk("Y", h0, h1) + tk("Y0", h0, h1) + tk("Y1", h0, h1))
+                continue
+            act(n("t%d" % k), ap("X", 3 * h0 + j, 3 * h1, 3), q(h0, h1), ACT.Tanh,
+                tk(qt, h0, h1), tk("X", h0, h1) + [n("new%d" % k)], bk, scale=0.625)
+            if k == 0 and not raz:
+                if cfg["xt"] == "G":
+                    cp(n("xt"), "G", ap("X", L + j, WE, 3), ap("X", j, TL, 3), tk("X", 0, 64), ["X.t"], n=TL // 3)
+                else:
+                    act(n("t0"), ap("X", L + j, WE, 3), q(0, TL // 3), ACT.Tanh, tk(qt, 0, 64), ["X.t"], bk, scale=0.625)
+        if t in (RO - 3, RO - 2):
+            for k in range(2):
+                cp(n("YW"[k]), "G", ap("Y", 1536 * k + j, 1536 * k + 1536, 3), ap("X", 1536 * k + j, 1536 * k + 1536, 3),
+                   [n("new%d" % x) for x in range(len(uc) - 1) if uc[x] < 512 * k + 512 and uc[x + 1] > 512 * k], tk("Y%d" % j, 512 * k, 512 * k + 512), n=512)
         if raz:
-            cp("xX%d" % m, "V", ind("X", 0, WW, "sl", 32 * m, 32 * m + 20), ap("lX", 480 * m, 480 * m + 320), 320,
-               ["lX%d" % m, "sl%d_0" % m, "sl%d_1" % m], XT, kind="x")
-            if cfg["x2"] == "V":
-                cp("xY%d" % m, "V", ind("X", 0, WW, "sl", 32 * m + 20, 32 * m + 30), ap("lX", c0, c0 + 160), 160,
-                   ["lY%d" % m, "sl%d_2" % m], XT, kind="x")
+            if "P" in ue:
+                cp(n("gY"), "A", ap("mX", c0, c0 + 160), ind("X", 0, WG, "gl", 32 * m + 20, 32 * m + 30),
+                   XT + [n("gl2")], [n("mY")])
+            send(n("sY"), ap("lX", c0, c0 + 160), ap("mX", c0, c0 + 160), "ry%d" % m, [n("mY")], [n("lY")])
+            cp(n("xX"), "V", ind("X", 0, WW, "sl", 32 * m, 32 * m + 20), ap("lX", 480 * m, 480 * m + 320),
+               [n("lX"), n("sl0"), n("sl1")], XT)
+            if cfg["xy"] == "V":
+                cp(n("xY"), "V", ind("X", 0, WW, "sl", 32 * m + 20, 32 * m + 30), ap("lX", c0, c0 + 160), [n("lY"), n("sl2")], XT)
             else:
-                act("xY%d" % m, ind("X", 0, WW, "sl", 32 * m + 20, 32 * m + 30), ap("lX", c0, c0 + 160), ACT.Tanh, 160,
-                    ["lY%d" % m, "sl%d_2" % m], XT, kind="x")
-            cp("xXt%d" % m, "A", ap("X", L, WE), ap("X", 0, TL), TL, tk("X", 0, 128), ["X.t"])
+                act(n("xY"), ind("X", 0, WW, "sl", 32 * m + 20, 32 * m + 30), ap("lX", c0, c0 + 160), ACT.Tanh, [n("lY"), n("sl2")], XT)
+            cp(n("xXt"), "A", ap("X", L, WE), ap("X", 0, TL), tk("X", 0, 64), ["X.t"])
 
     lists(0)
     for t in range(RO):
         control(t)
-        if t == 0:
-            mm("th", [(ap("SM", 272, 275), ap("E", 0, 128, p=8), ap("thb", 0, 3, p=8), True, True, 64)], ["E", "thb"], ["SM4"], ["SM"])
-            cp("thf", "V", ap("thf", 0, 3), ap("SM", 272, 275), 3, ["SM4"], ["thf"], ["SM"])
         if t % 3 == 2 and t < RO - 1:
-            razor_control(t // 3)
+            razor_control(t)
         signal(t)
-    mm("yc", [(ap("SM", 288, 480), Wr[r], ap("C", 192 * r, 192 * r + 192), r == 0, r == 15, 192) for r in range(16)],
-       ["Z"] + tk("C", 0, K), ["SM5"], ["SM"])
-    cp("ycs", "A", ap("ycs", 0, 192), ap("SM", 288, 480), 192, ["SM5"], ["ycs"], ["SM"])
-    store("stC", lambda T: T.yc[:], ap("ycs", 0, 192), 768, ["ycs"])
-    pe = ap("P", 64 * RO, 64 * RO + 64)
-    ts("pq", ap("pq", 0, 64), pe, 16.0 * L - 128 * RO, -16.0 * L, ALU.is_ge, ALU.mult, 64, ["P12"], ["pq"])
-    tt("pw0", ap("pw", 0, 64), pe, ap("pq", 0, 64), ALU.add, 64, ["P12", "pq"], ["pw0"])
-    ts("pw1", ap("pw", 64, 128), ap("pw", 0, 64), 128.0 * RO, None, ALU.add, None, 64, ["pw0"], ["pw1"])
-    ts("pi0", ap("pi", 0, 64), ap("pw", 64, 128), 8, None, ALU.arith_shift_right, None, 64, ["pw1"], ["pi0"])
-    ts("pi1", ap("pi", 64, 128), ap("pw", 64, 128), 255, None, ALU.bitwise_and, None, 64, ["pw1"], ["pi1"])
-    cp("pf", "V", ap("pf", 0, 128), ap("pi", 0, 128), 128, ["pi0", "pi1"], ["pf"])
-    store("stP", lambda T: T.yp[:], ap("pf", 0, 128), 512, ["pf"])
+    act("ycs", ap("ycs", 0, 192), ps(SR, 192), ACT.Identity, ["yc"], ["ycs"], [7], bias=QS)
+    store("stC", lambda T: T.yc[:], ap("ycs", 0, 192), ["ycs"])
+    pe, back = ap("P", 64 * RO, 64 * RO + 64), QS * (RO - 1)
+    ts("pq", ap("pq", 0, 64), pe, 16.0 * L - back, -16.0 * L, ALU.is_ge, ALU.mult, ["P12"], ["pq"])
+    tt("pw0", ap("pw", 0, 64), pe, ap("pq", 0, 64), ALU.add, ["P12", "pq"], ["pw0"])
+    ts("pw1", ap("pw", 64, 128), ap("pw", 0, 64), back, None, ALU.add, None, ["pw0"], ["pw1"])
+    ts("pi", ap("pi", 0, 64), ap("pw", 64, 128), 8, None, ALU.arith_shift_right, None, ["pw1"], ["pi0"])
+    ts("pi", ap("pi", 64, 128), ap("pw", 64, 128), 255, None, ALU.bitwise_and, None, ["pw1"], ["pi1"])
+    cp("pf", "V", ap("pf", 0, 128), ap("pi", 0, 128), ["pi0", "pi1"], ["pf"])
+    store("stP", lambda T: T.yp[:], ap("pf", 0, 128), ["pf"])
     return ops
 
 
-MODEL = {"cyc": 1.0, "pe": 0.5, "gi": 1.56, "sx": 3.5, "fv": 50.0, "fa": 65.0, "fp": 60.0, "sem": 80.0,
-         "iss": 600.0, "isq": 100.0, "up": 1800.0, "rate": 15.0, "row": 40.0, "wake": 200.0}
-
-
-def cost(op, md):
-    return sum(cost1(op, k, n, md) for k, n in op["cost"])
-
-
-def cost1(op, k, n, md):
-    if k == "p":
-        return md["fp"] + n * md["pe"]
-    if k == "g":
-        return 150.0 + 2 * n * md["cyc"]
-    if k == "q":
-        return md["isq"]
-    if k == "r":
-        return md["iss"]
-    f = {"v": 1.0, "h": 0.5, "i": md["gi"], "x": md["sx"]}[k]
-    return (md["fv"] if op["eng"] == "V" else md["fa"]) + max(64.0, n * f) * md["cyc"]
-
-
-def xfer(op, md):
-    return 8 * (md["row"] + op["dma"][2] / md["rate"])
-
-
-def run(ops, seq, md):
-    free, done, start, dma = {}, {}, {}, [0.0]
-    for n in seq:
-        op = ops[n]
-        s = free.get(op["eng"], 0.0)
-        for x in op["deps"]:
-            s = max(s, done[x])
-        start[n] = s
-        e = s + cost(op, md)
-        free[op["eng"]] = e
-        if op["dma"]:
-            dma[0] = max(e + md["up"], dma[0]) + xfer(op, md)
-            done[n] = dma[0] + md["wake"]
-        else:
-            done[n] = e + md["sem"]
-    return start, done
-
-
-def order(ops, cfg, md):
-    n = len(ops)
-    succ = [[] for x in range(n)]
-    for i, op in enumerate(ops):
-        for x in op["deps"]:
-            succ[x].append(i)
-    lv = [0.0] * n
-    rs = cfg["seed"] * 7919 + 12345
-    for i in range(n - 1, -1, -1):
-        op = ops[i]
-        c = cost(op, md) + (md["up"] + xfer(op, md) + md["wake"] if op["dma"] else md["sem"])
-        lv[i] = c + max([lv[x] for x in succ[i]] + [0.0])
-    pr = []
-    for i in range(n):
-        rs = (rs * 1103515245 + 12345) % 2147483648
-        pr.append(lv[i] + cfg["noise"] * (rs / 2147483648.0))
-    left = [len(op["deps"]) for op in ops]
-    cand = {i: 0.0 for i in range(n) if left[i] == 0}
-    free, done, dma, seq = {}, {}, 0.0, []
-    while cand:
-        best = min(cand, key=lambda i: (max(cand[i], free.get(ops[i]["eng"], 0.0)), -pr[i]))
-        e = ops[best]["eng"]
-        lim = max(cand[best], free.get(e, 0.0)) + cfg["delta"]
-        best = max([i for i in cand if ops[i]["eng"] == e and cand[i] <= lim], key=lambda i: pr[i])
-        op = ops[best]
-        f = max(cand.pop(best), free.get(e, 0.0)) + cost(op, md)
-        free[e] = f
-        if op["dma"]:
-            dma = max(f + md["up"], dma) + xfer(op, md)
-            done[best] = dma + md["wake"]
-        else:
-            done[best] = f + md["sem"]
-        seq.append(best)
-        for x in succ[best]:
-            left[x] -= 1
-            if left[x] == 0:
-                cand[x] = max(done[y] for y in ops[x]["deps"])
-    return seq
+def sequence(ops, head, cycle, last):
+    seq = head.split()
+    for base, names in ((0, cycle), (3, cycle), (6, cycle), (9, last)):
+        for e in names.split():
+            i = max(e.find("+"), e.find("-"))
+            seq.append(e if i < 0 else "%s.%d" % (e[:i], base + int(e[i:])))
+    return [e for e in seq if e in ops]
 
 
 def waits(ops, seq):
-    count, mark, snap, clock, out = {}, {}, {}, {}, {}
+    count, mark, snap, clock, out, bank, place = {}, {}, {}, {}, {}, {}, {}
     for n in seq:
         op = ops[n]
+        place[n] = len(place)
+        deps = set(x for x in op["deps"] if op["eng"] != "P" or ops[x]["eng"] != "P")
+        for b in op["b"]:
+            st = bank.setdefault(b, [op["eng"], [], []])
+            if st[0] != op["eng"]:
+                st[0], st[2], st[1] = op["eng"], st[1], []
+            deps.update(st[2])
+            st[1].append(n)
         ck = clock.setdefault(op["eng"], {})
         need = {}
-        for x in op["deps"]:
-            s, v = mark[x]
+        for x in deps:
+            s, v = (ops[x]["dma"][2], 16) if x in op["left"] else mark[x]
             if need.get(s, (0, 0))[0] < v:
                 need[s] = (v, x)
         ws = []
-        for s, (v, x) in sorted(need.items(), key=lambda e: -e[1][1]):
+        for s, (v, x) in sorted(need.items(), key=lambda e: -place[e[1][1]]):
             if ck.get(s, 0) < v:
                 ws.append((s, v))
-                for s2, v2 in snap[x].items():
+                for s2, v2 in ({s: v} if x in op["left"] else snap[x]).items():
                     if ck.get(s2, 0) < v2:
                         ck[s2] = v2
         out[n] = ws
@@ -561,27 +481,22 @@ def waits(ops, seq):
         mark[n] = (s, count[s])
         if op["dma"] and op["dma"][0] == "remote":
             snap[n] = {s: count[s]}
-            count["sent"] = count.get("sent", 0) + 16
+            count[op["dma"][2]] = count.get(op["dma"][2], 0) + 16
         else:
             snap[n] = dict(ck)
             snap[n][s] = count[s]
-    return out, mark, count
+    return out, count
 
 
 CACHE = {}
 
 
-def program():
+def emit(g, T, nx):
     if "p" not in CACHE:
         ops = plan(CFG)
-        al = "0123456789abcdefghijklmnopqrstuv"
-        seq = [al.index(ORDER[i]) * 32 + al.index(ORDER[i + 1]) for i in range(0, len(ORDER), 2)] or order(ops, CFG, MODEL)
+        seq = sequence(ops, HEAD, CYCLE, LAST)
         CACHE["p"] = (ops, seq) + waits(ops, seq)
-    return CACHE["p"]
-
-
-def emit(g, T, nx):
-    ops, seq, ws, mark, count = program()
+    ops, seq, ws, count = CACHE["p"]
     qs = {"V": g.vector, "A": g.scalar, "P": g.tensor, "G": g, "S": g.sync}
     for n in seq:
         op = ops[n]
@@ -593,7 +508,7 @@ def emit(g, T, nx):
             ins.then_inc(T.sem[op["eng"]], 1)
         elif op["dma"][0] == "local":
             ins.then_inc(T.sem[op["dma"][1]], 16)
-    for s in ("V", "A", "P", "G", "sent", "st"):
+    for s in [x for x in count if x[:4] == "left"] + ["V", "A", "P", "G", "sent", "st"]:
         g.wait_ge(T.sem[s], count[s])
 
 

from concourse.bass import DstId, RemoteDMATransfer
from concourse.mybir import AluOpType as ALU, ActivationFunctionType as ACT

K, L, RO, CAP = 1024, 3072, 12, 160
TL = 168
WE = L + TL
NB = 76
SP = K + CAP
WG, WW = 3 * SP, 6 * SP
QB = 192.0
QS = 16 * 16 * QB
F32, BF, I32, U16 = "float32", "bfloat16", "int32", "uint16"
PH, TP, SR, SM = 0, 2048, 3584, 3840

A3, H2, E4 = [0, 256, 512, K], [0, 512, K], [0, 192, 512, 832, K]
CFG = {"sp": {"s": {"ad": A3, "zb": [0, 512], "uc": H2, "ue": "VV", "ms": H2, "sz": H2},
              "r": {"ad": A3, "zb": [0, 512], "uc": H2, "ue": "VF", "ms": H2, "sz": H2},
              "o": {"ad": A3, "zb": [0, 512], "uc": H2, "ue": "FF", "ms": H2, "sz": H2},
              "x": {"ad": E4, "zb": [0, 512], "uc": E4, "ue": "VVFF", "ms": E4, "sz": []}},
       "steps": "srosrosrosrx", "slot": [0, 1, 2, 3] * 3, "xv": [""] * 12, "cv": [""] * 12, "red": (6, 7, 8, 9, 10, 11),
       "xy": "V", "qa": (), "sc": [("C", 0, 30)], "xct": "A", "ct": "A", "xt": "A", "ms": "A"}

HEAD = """
ki ki1 kf mk kl0 ldP nil ldC xrow NI kl ZN Z v.0 NU0 ID to0.0 ldCt IF blk B0 ldX kb E w.0 ldT to1.0 BD B1 ldXt one cv2.0 x1.0 cv1.0
tx1.0 x0.0 cn1.0 tx0.0 cn0.0 cx.0 ZR p.0 a0.0 a1.0 th0 v.1 x1.1 x0.1 a2.0 th1 f.0 NU d0.0 w.1 to0.1 ph1.0 th2 ph0.0 to1.1 tx1.1 d1.0
q1.1 m0.0 q0.1 cx.1 tx0.1 cq.1 s0.0 f.1 p.1 v.2 th3
"""
CYCLE = """
cn1+1 cn0+1 x0+2 d2+0 m1+0 q0+2 s1+0 to1+2 ro1+0 x1+2 q1+2 to0+2 tx0+2 tx1+2 ph1+1 u1+0 sz0+0 cn0+2 cn1+2 u0+0 r0+2 r1+2 t1+0 Sn+2
Sq+2 w+2 cut+2 inc+2 M+2 sz1+0 t0+0 a0+1 a1+1 ph0+1 MS+2 d0+1 d1+1 J0+2 J1+2 m0+1 sn+2 s0+1 J16+2 sz0+1 ro0+1 cmp+2 u0+1 Jb+2 R+2 gl+2
a2+1 ia1+1 ro1+1 d2+1 gC+2 m1+1 iv+2 y+2 u1+1 cx+2 cq+2 t0+1 t1+1 sC+2 sl+2 f+2 gid+2 p+2 w+3 a0+2 d0+2 ph1+2 sz1+1 a1+2 ph0+2 gX+2
a2+2 ia0+2 v+3 d1+2 m0+2 xC+2 ro0+2 ia1+2 d2+2 m1+2 u0+2 ro1+2 u1+2 xCt+2 x0+3 x1+3 q0+3 to0+3 to1+3 cx+3 q1+3 gY+2 sX+2 tx0+3 sz0+2
f+3 cq+3 t0+2 p+3 t1+2 cn0+3 w+4 v+4 f+4 xX+2 tx1+3 cn1+3 x1+4 sY+2 xY+2 ph0+3 to0+4 to1+4 x0+4 ro0+3 sz1+2 q0+4 q1+4 xXt+2 a1+3 a0+3
cx+4 d1+3 d0+3 tx1+4 cq+4 m0+3 p+4 s0+3 v+5 tx0+4 ph1+3 a2+3
"""
LAST = """
d2+0 u0+0 cn1+1 cn0+1 x1+2 x0+2 ro1+0 sz0+0 m1+0 s1+0 ph0+1 to0+2 to1+2 cx+2 t0+0 u1+0 t1+0 a0+1 ph1+1 a1+1 q0+2 w+2 q1+2 tx0+2 tx1+2
ro0+1 a2+1 cn1+2 sz1+0 ia1+1 r1+0 d0+1 d1+1 m0+1 s0+1 Y+0 ro1+1 sz0+1 d2+1 f+2 m1+1 u0+1 u1+1 cq+2 ph0+2 ph1+2 t0+1 sz1+1 p+2 t1+1 pq
r0+0 r0+1 pw0 pw1 a0+2 r1+1 d0+2 pi m0+2 pf s0+2 a3+2 stP a1+2 d1+2 Sn+0 Sq+0 ro0+2 a2+2 ia1+2 u0+2 m1+2 s1+2 u1+2 ro1+2 t0+2 cn0+2
d2+2 m2+2 r1+2 u2+2 d3+2 W+1 Y+1 m3+2 r0+2 u3+2 Sn+1 Sq+1 t1+2 st0+2 W+0 t2+2 st1+2 t3+2 Sn+2 Sq+2 st2+2 ycs st3+2 stC
"""

SCRATCH = {
    "rawX": ("sbuf", [128, L + 176], BF),
    "X": ("sbuf", [128, WW], F32), "C": ("sbuf", [128, WW], BF), "Y": ("sbuf", [128, L], F32),
    "P": ("sbuf", [128, 13 * 64], I32), "v16": ("sbuf", [128, 12 * 64], U16), "w16": ("sbuf", [128, 12 * 64], U16),
    "lo": ("sbuf", [128, 12 * 64], I32), "ph": ("sbuf", [128, 12 * 128], BF),
    "xb": ("sbuf", [128, 2 * K], BF), "qb": ("sbuf", [128, 2 * K], BF), "qn": ("sbuf", [128, 2 * K], BF),
    "a": ("sbuf", [128, 4 * K], F32), "u": ("sbuf", [128, 2 * K], F32),
    "s": ("sbuf", [128, 12 * K], F32), "z": ("sbuf", [128, 11 * K], F32),
    "xrow": ("sbuf", [128, 256], F32), "blk": ("sbuf", [128, 128], F32), "ki": ("sbuf", [128, 4], I32),
    "kf": ("sbuf", [128, 8], F32), "kl0": ("sbuf", [128, 16], F32), "kl": ("sbuf", [128, 16], F32), "kb": ("sbuf", [128, 16], F32),
    "Z": ("sbuf", [128, 144], BF), "ZN": ("sbuf", [128, 144], BF), "B": ("sbuf", [128, 1024], BF), "BD": ("sbuf", [128, 128], BF),
    "NU0": ("sbuf", [128, 128], BF), "NU": ("sbuf", [128, 128], BF), "ID": ("sbuf", [128, 128], BF),
    "NI": ("sbuf", [128, 128], BF), "ZR": ("sbuf", [128, 256], F32), "E": ("sbuf", [128, 128], BF), "IF": ("sbuf", [128, 128], F32),
    "thi": ("sbuf", [128, 4], I32), "thf0": ("sbuf", [128, 4], F32), "thb": ("sbuf", [128, 8], BF), "thf": ("sbuf", [128, 4], F32),
    "cut": ("sbuf", [128, 240], BF), "inc": ("sbuf", [128, 240], BF), "MS": ("sbuf", [128, 288], F32),
    "junk": ("sbuf", [128, 800], BF), "JS": ("sbuf", [128, 48], F32), "J16": ("sbuf", [128, 48], U16),
    "Jb": ("sbuf", [128, 48], BF), "cmp": ("sbuf", [128, 480], BF),
    "gl": ("sbuf", [128, 96], U16), "sl": ("sbuf", [128, 96], U16), "gid": ("sbuf", [128, 48], U16),
    "nb": ("sbuf", [128, 12], F32), "iv": ("sbuf", [128, 48], F32), "y": ("sbuf", [128, 48], F32),
    "mC": ("sbuf", [128, 1440], BF), "lC": ("sbuf", [128, 1440], BF),
    "mX": ("sbuf", [128, 1440], F32), "lX": ("sbuf", [128, 1440], F32),
    "ycs": ("sbuf", [128, 192], F32), "pq": ("sbuf", [128, 64], F32), "pw": ("sbuf", [128, 128], I32),
    "pi": ("sbuf", [128, 128], I32), "pf": ("sbuf", [128, 128], F32),
    "PS": ("psum", [128, 4096], F32),
}
SEMAPHORES = (["V", "A", "P", "G", "sent", "st", "l0", "l1", "l2", "l3", "l4", "l5"]
              + ["%sz%d_%d" % (x, t, k) for t in range(11) for k in range(3) for x in ("", "left")]
              + ["r%s%d" % (x, m) for x in "ncdxy" for m in range(3)])


def plan(cfg):
    ops, lastw, readers = {}, {}, {}

    def add(name, eng, fn, r=(), w=(), b=(), dma=None, grp=""):
        op = ops.setdefault(name, {"name": name, "eng": eng, "fn": [], "deps": set(), "left": set(), "b": set(), "dma": dma, "grp": grp})
        op["fn"].append(fn)
        op["b"].update(b)
        for k in list(r) + list(w):
            if k in lastw:
                op["deps"].add(lastw[k])
        for k in w:
            op["deps"].update(readers.get(k, ()))
            op["left"].update(x for x in readers.get(k, ()) if ops[x]["dma"] and ops[x]["dma"][0] == "remote")
        for k in r:
            readers.setdefault(k, []).append(name)
        for k in w:
            lastw[k] = name
            readers[k] = []
        op["deps"].discard(name)

    def tk(p, h0, h1):
        return ["%s.%d" % (p, i) for i in range(h0 // 64, (h1 + 63) // 64)]

    def ts(name, out, in0, s1, s2, op0, op1, r, w, b=()):
        def fn(g, T, nx):
            x1 = s1(T) if not isinstance(s1, (int, float)) else s1
            if s2 is None:
                return g.vector.tensor_scalar(out(T), in0(T), x1, None, op0)
            x2 = s2(T) if not isinstance(s2, (int, float)) else s2
            return g.vector.tensor_scalar(out(T), in0(T), x1, x2, op0, op1)
        add(name, "V", fn, r, w, b)

    def tt(name, out, in0, in1, op, r, w, b=()):
        add(name, "V", lambda g, T, nx: g.vector.tensor_tensor(out(T), in0(T), in1(T), op), r, w, b)

    def cp(name, eng, out, in_, r, w, b=(), n=0):
        if eng == "V":
            add(name, "V", lambda g, T, nx: g.vector.tensor_copy(out(T), in_(T)), r, w, b)
        elif eng == "G":
            add(name, "G", lambda g, T, nx: g.affine_select(out(T), in_(T), [[0, n]], ALU.is_ge, 0.0, 0, 0), r, w)
        else:
            act(name, out, in_, ACT.Identity, r, w, b)

    def act(name, out, in_, func, r, w, b=(), **kw):
        add(name, "A", lambda g, T, nx: g.scalar.activation(out(T), in_(T), func, **kw), r, w, b)

    def mm(name, lst, r, w, b, grp="oc"):
        def fn(g, T, nx):
            for o, l, x, s0, s1 in lst:
                ins = g.tensor.matmul(o(T), l(T), x(T), s0, s1)
            return ins
        add(name, "P", fn, r, w, b, grp=grp)

    def ap(buf, a, z, step=1, p=None):
        if p is None:
            return lambda T: T[buf][:, a:z:step] if step != 1 else T[buf][:, a:z]
        return lambda T: T[buf][0:p, a:z]

    def ps(a, n, step=1):
        return ap("PS", a, a + n, step)

    def ind(buf, a, z, off, c0, c1):
        return lambda T: T[buf][:, a:z].indirect(T[off][:, c0:c1])

    def load(name, q, out, in_, sem, w):
        add(name, q, lambda g, T, nx: (g.sync if q == "S" else g.scalar).dma_start(out(T), in_(T)), (), w, dma=("local", sem))

    def store(name, out, in_, r):
        add(name, "S", lambda g, T, nx: g.sync.dma_start(out(T), in_(T)), r, (), dma=("local", "st"))

    def send(name, out, in_, sem, r, w, in2=None):
        if in2 is None:
            add(name, "G", lambda g, T, nx: g.remote_dma(out(T), in_(T), T.sem[sem], T.sem["sent"], nx[0], nx[1], nx[2]),
                r, w, dma=("remote", sem, "sent"))
        else:
            add(name, "G", lambda g, T, nx: g.remote_dma_fused(
                [RemoteDMATransfer(dst_ids=[DstId(rid=nx[1], pnc=nx[0])], dma_engine_mask=nx[2], remote_sem=T.sem[sem],
                                   srcs=[in_(T), in2(T)], dsts=[out(T)], alu_op=1)], local_sem=T.sem["left" + sem]),
                r, w, dma=("remote", sem, "left" + sem))

    def iota(name, out, pat, cm, w, flt=True):
        if flt:
            add(name, "G", lambda g, T, nx: g.iota(out(T), pat, 0, cm, allow_small_or_imprecise_dtypes=True), (), w)
        else:
            add(name, "G", lambda g, T, nx: g.iota(out(T), pat, 0, cm), (), w)

    Wr = [ap("Z", 15 - r, 143 - r) for r in range(16)]
    Wn = [ap("ZN", 15 - r, 143 - r) for r in range(16)]
    ID, NI, IF, BD, NU = [ap(x, 0, 128) for x in ("ID", "NI", "IF", "BD", "NU")]
    kf = [ap("kf", i, i + 1) for i in range(8)]
    XT = tk("X", 0, K) + ["X.t", "X.p1", "X.p2", "X.s"]
    CP = [["C%d.0" % j, "C%d.1" % j] for j in range(3)]
    CT = CP[0] + CP[1] + CP[2] + ["C.t"]

    load("ldP", "A", ap("P", 0, 64), lambda T: T.pos[:], "l0", ["P0"])
    load("ldC", "S", ap("C", 0, L), lambda T: T.ctl[:], "l1", CT[:6])
    load("ldX", "S", ap("rawX", 0, L), lambda T: T.tape[:], "l2", ["rawX"])
    load("ldCt", "A", ap("C", L, WG), lambda T: T.ctl[:, 0:WG - L], "l3", ["C.t"])
    load("ldXt", "A", ap("rawX", L, L + 176), lambda T: T.tape[:, 0:176], "l4", ["rawXt"])
    load("ldT", "S", ap("thi", 0, 3, p=8), lambda T: T.th[:], "l5", ["thi"])
    iota("ki", ap("ki", 0, 1), [[0, 1]], 1, ["ki0"], False)
    iota("xrow", ap("xrow", 0, 256), [[1, 256]], 0, ["xrow"])
    iota("blk", ap("blk", 0, 128), [[16, 8], [0, 16]], 0, ["blk"])
    iota("kl0", ap("kl0", 0, 10), [[16, 10]], 1, ["kl0"])
    for i, mk in ((1, 0x70), (2, 0x77), (3, 8)):
        ts("ki1", ap("ki", i, i + 1), ap("ki", 0, 1), mk, None, ALU.bitwise_and, None, ["ki0"], ["ki%d" % i])
    cp("kf", "V", ap("kf", 0, 4), ap("ki", 0, 4), ["ki0", "ki1", "ki2", "ki3"], ["kf"])
    ts("mk", kf[4], kf[3], 0.0, 0.0625, ALU.is_equal, ALU.mult, ["kf"], ["mk0"])
    ts("mk", kf[5], kf[3], 1.0 / 128, None, ALU.mult, None, ["kf"], ["mk1"])
    ts("mk", kf[6], kf[1], 15.0, None, ALU.add, None, ["kf"], ["pb15"])
    ts("Z", ap("Z", 0, 144), ap("xrow", 0, 144), kf[6], None, ALU.is_equal, None, ["xrow", "pb15"], ["Z"])
    ts("ZN", ap("ZN", 0, 144), ap("xrow", 0, 144), kf[6], -16.0, ALU.is_equal, ALU.mult, ["xrow", "pb15"], ["ZN"])
    ts("ID", ID, ap("xrow", 0, 128), kf[0], None, ALU.is_equal, None, ["xrow", "kf"], ["ID"])
    ts("NI", NI, ap("xrow", 0, 128), kf[0], -16.0, ALU.is_equal, ALU.mult, ["xrow", "kf"], ["NI"])
    ts("IF", IF, ap("xrow", 0, 128), kf[0], None, ALU.is_equal, None, ["xrow", "kf"], ["IF"])
    for r in range(8):
        ts("B%d" % (r // 4), ap("B", 128 * r, 128 * r + 128), ap("blk", 0, 128), float(r), kf[2], ALU.add, ALU.is_equal,
           ["blk", "kf"], ["B%d" % r])
    for h in range(2):
        ts("ZR", ap("ZR", 128 * h, 128 * h + 128), ap("xrow", 0, 128), kf[0], 0.6, ALU.is_equal, ALU.mult,
           ["xrow", "kf"], ["ZR%d" % h])
    ts("BD", BD, ap("blk", 0, 128), kf[1], None, ALU.is_equal, None, ["blk", "kf"], ["BD"])
    ts("NU0", ap("NU0", 0, 128), ap("xrow", 0, 128), kf[0], -1.0, ALU.is_lt, ALU.mult, ["xrow", "kf"], ["NU0"])
    tt("NU", NU, ap("NU0", 0, 128), BD, ALU.mult, ["NU0", "BD"], ["NU"])
    ts("kl", ap("kl", 0, 10), ap("kl0", 0, 10), kf[1], None, ALU.subtract, None, ["kl0", "kf"], ["kl"])
    ts("kb", ap("kb", 0, 10), ap("kl", 0, 10), 0.5, None, ALU.add, None, ["kl"], ["kb"])
    act("one", ap("cut", 0, 240), ap("xrow", 0, 240), ACT.Tanh, ["xrow"], ["one"], bias=16.0)
    add("nil", "V", lambda g, T, nx: g.vector.memset(T["X"][:, WE:WG], 0.0), (), ["X.s"])
    ts("E", ap("E", 0, 128, p=8), ap("blk", 0, 128, p=8), 0.0625, ap("kf", 0, 1, p=8), ALU.mult, ALU.is_equal,
       ["blk", "kf"], ["E"])
    cp("th0", "V", ap("thf0", 0, 3, p=8), ap("thi", 0, 3, p=8), ["thi"], ["thf0"])
    cp("th1", "V", ap("thb", 0, 3, p=8), ap("thf0", 0, 3, p=8), ["thf0"], ["thb"])
    mm("th2", [(ps(SR + 240, 3), ap("E", 0, 128, p=8), ap("thb", 0, 3, p=8), True, True)], ["E", "thb"], ["th"], [7])
    ts("th3", ap("thf", 0, 3), ps(SR + 240, 3), -QS, None, ALU.add, None, ["th"], ["thf"], [7])
    for j in (1, 2):
        cp("cv%d.0" % j, "G", ap("X", j, WE, 3), ap("rawX", j, WE, 3), ["rawX", "rawXt"], ["X.p%d" % j], n=WE // 3)

    def lists(t):
        c0 = 64 * t
        src, off, rd = ap("P", c0, c0 + 64), QS / 16 * max(t - 1, 0) - 0.46875, ["P%d" % t]
        ts("v.%d" % t, ap("v16", c0, c0 + 64), src, 0.0625, off, ALU.mult, ALU.add, rd, ["v%d" % t])
        ts("w.%d" % t, ap("w16", c0, c0 + 64), src, 0.0625, off + 1.0, ALU.mult, ALU.add, rd, ["w%d" % t])
        ts("w.%d" % t, ap("lo", c0, c0 + 64), src, 15, None, ALU.bitwise_and, None, rd, ["lo%d" % t])
        for h in range(2):
            ts("f.%d" % t, ap("ph", 128 * t + h, 128 * t + 128, 2), ap("lo", c0, c0 + 64), kf[4 + h], None, ALU.mult, None,
               ["lo%d" % t, "mk%d" % h], ["ph%d_%d" % (t, h)])

    def floor16(name, out, in_, r, w):
        if name in cfg["qa"]:
            act(name, out, in_, ACT.Identity, r, w, bias=QB - 0.46875, scale=0.0625)
        else:
            ts(name, out, in_, 0.0625, QB - 0.46875, ALU.mult, ALU.add, r, w)

    def plane_sums(t, dst, tok):
        j, o, qn = t % 3, K * (t % 2), "qn%d" % (t % 2)
        for h in range(2):
            floor16("r%d.%d" % (h, t), ap("qn", o + 512 * h, o + 512 * h + 512), ap("C", 1536 * h + j, 1536 * h + 1536, 3),
                    [CP[j][h]], tk(qn, 512 * h, 512 * h + 512))
        if t < RO - 3:
            x, q = [ap("C", 3 * r + j, L, 48) for r in range(16)], [ap("qn", o + r, o + K, 16) for r in range(16)]
        else:
            x = [ap("C", 192 * r + j, 192 * r + 192, 3) for r in range(16)]
            q = [ap("qn", o + 64 * r, o + 64 * r + 64) for r in range(16)]
        mm("Sn.%d" % t, [(dst, Wr[r], x[r], r == 0, False) for r in range(16)], ["Z"] + CP[j], [tok], [7], "o")
        mm("Sq.%d" % t, [(dst, Wn[r], q[r], False, r == 15) for r in range(16)], ["ZN"] + tk(qn, 0, K), [tok], [7], "c")

    def control(t):
        j, o = t % 3, K * (t % 2)
        xb, qb = "xb%d" % (t % 2), "qb%d" % (t % 2)
        red = t in cfg["red"]
        for h in range(2):
            h0, h1 = 512 * h, 512 * h + 512
            cp("x%d.%d" % (h, t), "V" if str(h) in cfg["xv"][t] else "A", ap("xb", o + h0, o + h1),
               ind("C", 0, WE if t else L, "v16", 64 * t + h0 // 16, 64 * t + h1 // 16), CT[:7 if t else 6] + ["v%d" % t], tk(xb, h0, h1))
            if t > 0:
                floor16("q%d.%d" % (h, t), ap("qb", o + h0, o + h1), ap("xb", o + h0, o + h1), tk(xb, h0, h1), tk(qb, h0, h1))
        mm("cx.%d" % t, [(ps(SM, 64), Wr[r], ap("xb", o + r, o + K, 16), r == 0, t == 0 and r == 15) for r in range(16)],
           ["Z"] + tk(xb, 0, K), ["SM"], [7], "o" if t else "oc")
        if t > 0:
            mm("cq.%d" % t, [(ps(SM, 64), Wn[r], ap("qb", o + r, o + K, 16), False, r == 15) for r in range(16)],
               ["ZN"] + tk(qb, 0, K), ["SM"], [7], "c")
        tt("p.%d" % t, ap("P", 64 * t + 64, 64 * t + 128), ps(SM, 64), ap("P", 64 * t, 64 * t + 64), ALU.add,
           ["SM", "P%d" % t], ["P%d" % (t + 1)], [7])
        if t < RO - 1:
            lists(t + 1)
        bias = 16 * QB if red else 0.0
        for h in range(2):
            h0, h1, tp = 512 * h, 512 * h + 512, "TP%d" % h
            old, dst = ap("C", 3 * h0 + j, 3 * h1, 3), ps(TP + h0, 512)
            mm("to%d.%d" % (h, t), [(dst, ID, old, True, False)], ["ID", CP[j][h]], [tp], [4 + h], "o")
            mm("tx%d.%d" % (h, t), [(dst, ID, ap("xb", o + h0, o + h1), False, not red)]
               + ([(dst, NI, ap("qb", o + h0, o + h1), False, True)] if red else []),
               ["ID", "NI"] + tk(xb, h0, h1) + (tk(qb, h0, h1) if red else []), [tp], [4 + h], "c")
        for h in range(2):
            h0, h1, tp = 512 * h, 512 * h + 512, "TP%d" % h
            name, new = "cn%d.%d" % (h, t), ap("C", 3 * h0 + j, 3 * h1, 3)
            if str(h) in cfg["cv"][t]:
                ts(name, new, ps(TP + h0, 512), bias, None, ALU.add, None, [tp], [CP[j][h]], [4 + h])
            else:
                act(name, new, ps(TP + h0, 512), ACT.Identity, [tp], [CP[j][h]], [4 + h], bias=bias)
            if h == 0 and t < RO - 1 and j != 2:
                if cfg["ct"] == "G":
                    cp("ct.%d" % t, "G", ap("C", L + j, WE, 3), ap("C", j, TL, 3), [CP[j][0]], ["C.t"], n=TL // 3)
                else:
                    act(name, ap("C", L + j, WE, 3), ps(TP, TL // 3), ACT.Identity, [tp], ["C.t"], [4], bias=bias)
        if t >= RO - 3:
            plane_sums(t, ps(SR + j, 192 - j, 3), "yc")

    def razor_control(t):
        m = t // 3
        c80, c16, c32, c96 = 80 * m, 16 * m, 32 * m, 96 * m
        n = lambda s: "%s.%d" % (s, t)
        plane_sums(t, ps(SR, 64), "S")
        cut, inc, cum, pre, ids = ap("cut", c80, c80 + NB), ap("inc", c80, c80 + NB), ps(SR + 64, NB), ps(SR + 64 + NB, NB), ps(SR + 224, 10)
        ts(n("cut"), ap("cut", c80, c80 + 64), ps(SR, 64), ap("thf", m, m + 1), None, ALU.is_ge, None, ["S", "thf", "one"], [n("cut")], [7])
        add(n("inc"), "V", lambda g, T, nx: g.vector.tensor_tensor_scan(inc(T), cut(T), cut(T), 0.0, ALU.add, ALU.max),
            [n("cut")], [n("inc")])
        mm(n("M"), [(cum, BD, inc, True, True), (pre, BD, inc, True, False), (pre, NU, cut, False, True)],
           ["BD", "NU", n("inc"), n("cut")], ["M"], [7])
        for kk in range(10):
            add(n("J%d" % (kk // 5)), "A", lambda g, T, nx, kk=kk: g.scalar.activation(
                T["junk"][:, 80 * kk:80 * kk + NB], cum(T), ACT.Sign,
                bias=T["kb"][:, kk:kk + 1], scale=-1.0, accum_out=T["JS"][:, c16 + kk:c16 + kk + 1]),
                ["M", "kb"], [n("JS%d" % kk), "junk%d" % kk], [7])
        cp(n("MS"), cfg["ms"], ap("MS", c96, c96 + NB + 16), ps(SR + 124, NB + 16), ["M"], [n("MS")], [7])
        send(n("sn"), ap("nb", 4 * m, 4 * m + 4), ap("MS", c96, c96 + 4), "rn%d" % m, [n("MS")], [n("nb")])
        js = [n("JS%d" % kk) for kk in range(10)]
        ts(n("J16"), ap("J16", c16, c16 + 10), ap("JS", c16, c16 + 10), 0.5, NB / 2, ALU.mult, ALU.add, js, [n("J16")])
        act(n("Jb"), ap("Jb", c16, c16 + 10), ap("JS", c16, c16 + 10), ACT.Identity, js, [n("Jb")], bias=8.0 * NB, scale=8.0)
        tt(n("cmp"), ap("cmp", 160 * m, 160 * m + 160), ind("MS", c96 + 16, c96 + 16 + NB, "J16", c16, c16 + 10), ap("xrow", 0, 160),
           ALU.is_le, [n("MS"), n("J16"), "xrow"], [n("cmp")])
        mm(n("R"), [(ids, ID, ap("Jb", c16, c16 + 10), True, False)]
           + [(ids, Wr[r], ap("cmp", 160 * m + r, 160 * m + 160, 16), False, r == 15) for r in range(16)],
           ["Z", "ID", n("Jb"), n("cmp")], ["R"], [7])
        for c in range(3):
            ts(n("gl"), ap("gl", c32 + 10 * c, c32 + 10 * c + 10), ids, 3.0, float(c), ALU.mult, ALU.add, ["R"], [n("gl%d" % c)], [7])
        if "P" not in cfg["sp"][cfg["steps"][t]]["ue"]:
            ts(n("gid"), ap("gid", c16, c16 + 10), ids, float(K - 1), None, ALU.min, None, ["R"], [n("gid")], [7])
        ts(n("iv"), ap("iv", c16, c16 + 10), ap("kl", 0, 10), ap("nb", 4 * m + 3, 4 * m + 4), float(SP), ALU.is_ge, ALU.mult,
           ["kl", n("nb")], [n("iv")])
        tt(n("y"), ap("y", c16, c16 + 10), ids, ap("iv", c16, c16 + 10), ALU.add, ["R", n("iv")], [n("y")], [7])
        for c in range(3):
            ts(n("sl"), ap("sl", c32 + 10 * c, c32 + 10 * c + 10), ap("y", c16, c16 + 10), 3.0, float(c), ALU.mult, ALU.add,
               [n("y")], [n("sl%d" % c)])
        gl, sl = [n("gl%d" % c) for c in range(3)], [n("sl%d" % c) for c in range(3)]
        for x, l0, l1 in cfg["sc"]:
            e0, e1 = 480 * m + 16 * l0, 480 * m + 16 * l1
            cp(n("g" + x), "A", ap("mC", e0, e1), ind("C", 0, WG, "gl", c32 + l0, c32 + l1), CT + gl, [n("m" + x)])
            send(n("s" + x), ap("lC", e0, e1), ap("mC", e0, e1), "r%s%d" % (x.lower(), m), [n("m" + x)], [n("l" + x)])
        for x, l0, l1 in cfg["sc"]:
            e0, e1 = 480 * m + 16 * l0, 480 * m + 16 * l1
            cp(n("x" + x), "V", ind("C", 0, WW, "sl", c32 + l0, c32 + l1), ap("lC", e0, e1), [n("l" + x)] + sl, CT)
        cp(n("xCt"), cfg["xct"], ap("C", L, WE), ap("C", 0, TL), [CP[0][0], CP[1][0], CP[2][0]], ["C.t"], n=TL)

    def signal(t):
        j, o, so, m = t % 3, K * (t % 2), K * t, t // 3
        raz, end = j == 2 and t < RO - 1, t == RO - 1
        n = lambda s: "%s.%d" % (s, t)
        a, u, s = "a%d" % (t % 2), "u%d" % (t % 2), "s%d" % t
        win, rd = ("rawX", ["rawX", "rawXt"]) if t == 0 else ("X", XT)
        for b in range(2):
            mm(n("ph%d" % b), [(ps(PH + 512 * b + r, 512 - r, 8), ap("B", 128 * r, 128 * r + 128),
                                ap("ph", 128 * t + 64 * b, 128 * t + 64 * b + 64), True, True) for r in range(8)],
               ["B%d" % r for r in range(8)] + ["ph%d_0" % t, "ph%d_1" % t], tk("PH", 512 * b, 512 * b + 512), [b])
        sp = cfg["sp"][cfg["steps"][t]]
        ad, uc, ue = sp["ad"], sp["uc"], sp["ue"] if t else "VVVV"
        slot = cfg["slot"][t]
        a, ao = "a%d" % slot, K * slot
        for k in range(len(ad) - 1):
            h0, h1 = ad[k], ad[k + 1]
            l0, l1 = 64 * t + h0 // 16, 64 * t + h1 // 16
            cp(n("a%d" % k), "A", ap("a", ao + h0, ao + h1), ind(win, 0, WE if t else L, "v16", l0, l1), rd[:None if t else 1] + ["v%d" % t], tk(a, h0, h1))
            tt(n("d%d" % k), ap("s", so + h0, so + h1), ind(win, 0, WE, "w16", l0, l1), ap("a", ao + h0, ao + h1), ALU.subtract,
               rd + ["w%d" % t] + tk(a, h0, h1), tk(s, h0, h1))
        banks = list(zip(sp["zb"], (2, 3, 6)))
        zb = lambda h: max(e for e in banks if e[0] <= h)
        zp = lambda h0, h1: ps(512 * zb(h0)[1] + h0 - zb(h0)[0], h1 - h0)
        kind = lambda h: ue[max(k for k in range(len(uc) - 1) if uc[k] <= h)]
        if t > 0:
            sh = 16 * (t % 8)
            for b, (h0, bk) in enumerate(banks):
                h1, x = (banks + [(K, 0)])[b + 1][0], kind(h0)
                if x == "F":
                    mm(n("ia%d" % b), [(zp(h0, h1), IF, ap("a", ao + h0, ao + h1), True, False)],
                       ["IF"] + tk(a, h0, h1), tk("ZP", h0, h1), [bk], "o")
                mm(n("ro%d" % b), [(zp(h0, h1), ap("ZR", sh, sh + 128), ap("z", so - K + h0, so - K + h1), x != "F", x != "P")],
                   ["ZR0", "ZR1"] + tk("z%d" % (t - 1), h0, h1), tk("ZP", h0, h1), [bk], {"P": "o", "V": "oc", "F": "c"}[x])
        if raz:
            cp(n("gX"), "A", ap("mX", 480 * m, 480 * m + 320), ind("X", 0, WG, "gl", 32 * m, 32 * m + 20),
               XT + [n("gl0"), n("gl1")], [n("mX")])
            send(n("sX"), ap("lX", 480 * m, 480 * m + 320), ap("mX", 480 * m, 480 * m + 320), "rx%d" % m, [n("mX")], [n("lX")])
        ms, sz = sp["ms"], sp["sz"]
        for k in range(len(ms) - 1):
            h0, h1 = ms[k], ms[k + 1]
            f, sk, bk = ps(PH + h0, h1 - h0), ap("s", so + h0, so + h1), sorted({h0 // 512, (h1 - 1) // 512})
            if kind(h0) == "F":
                tt(n("m%d" % k), sk, sk, f, ALU.mult, tk(s, h0, h1) + tk("PH", h0, h1), tk(s, h0, h1), bk)
                continue
            tt(n("m%d" % k), f, sk, f, ALU.mult, tk(s, h0, h1) + tk("PH", h0, h1), tk("PH", h0, h1), bk)
            tt(n("s%d" % k), sk, f, ap("a", ao + h0, ao + h1), ALU.add, tk(a, h0, h1) + tk("PH", h0, h1), tk(s, h0, h1), bk)
        for k in range(len(sz) - 1):
            h0, h1 = sz[k], sz[k + 1]
            fo = kind(h0) == "F"
            send(n("sz%d" % k), ap("z", so + h0, so + h1), ap("s", so + h0, so + h1), "z%d_%d" % (t, k),
                 tk(s, h0, h1) + (tk(a, h0, h1) if fo else []), tk("z%d" % t, h0, h1), ap("a", ao + h0, ao + h1) if fo else None)
        src, sof, st = ("s", so, s) if t == 0 else ("u", o, u)
        for k in range(len(uc) - 1 if t else 0):
            h0, h1 = uc[k], uc[k + 1]
            if ue[k] != "P":
                tt(n("u%d" % k), ap("u", o + h0, o + h1), zp(h0, h1), ap("s", so + h0, so + h1), ALU.add,
                   tk(s, h0, h1) + tk("ZP", h0, h1), tk(u, h0, h1), [zb(h0)[1]])
            else:
                mm(n("u%d" % k), [(zp(h0, h1), IF, ap("s", so + h0, so + h1), False, True)],
                   ["IF"] + tk(s, h0, h1), tk("ZP", h0, h1), [zb(h0)[1]], "c")
        c0 = 480 * m + 320
        if raz and "P" not in ue:
            act(n("gY"), ap("mX", c0, c0 + 160), ind("u", o, o + K, "gid", 16 * m, 16 * m + 10), ACT.Tanh if cfg["xy"] == "V" else ACT.Identity,
                tk(u, 0, K) + [n("gid")], [n("mY")], scale=0.625)
        for k in range(len(uc) - 1):
            h0, h1 = uc[k], uc[k + 1]
            pe = t > 0 and ue[k] == "P"
            q = zp if pe else (lambda x0, x1: ap(src, sof + x0, sof + x1))
            qt, bk = ("ZP", [zb(h0)[1]]) if pe else (st, [])
            if end:
                act(n("t%d" % k), ap("Y", 3 * h0 + j, 3 * h1, 3), q(h0, h1), ACT.Tanh, tk(qt, h0, h1), tk("Y", h0, h1), bk, scale=0.625)
                store(n("st%d" % k), lambda T, h0=h0, h1=h1: T.yx[:, 3 * h0:3 * h1], ap("Y", 3 * h0, 3 * h1),
                      tk("Y", h0, h1) + tk("Y0", h0, h1) + tk("Y1", h0, h1))
                continue
            act(n("t%d" % k), ap("X", 3 * h0 + j, 3 * h1, 3), q(h0, h1), ACT.Tanh,
                tk(qt, h0, h1), tk("X", h0, h1) + [n("new%d" % k)], bk, scale=0.625)
            if k == 0 and not raz:
                if cfg["xt"] == "G":
                    cp(n("xt"), "G", ap("X", L + j, WE, 3), ap("X", j, TL, 3), tk("X", 0, 64), ["X.t"], n=TL // 3)
                else:
                    act(n("t0"), ap("X", L + j, WE, 3), q(0, TL // 3), ACT.Tanh, tk(qt, 0, 64), ["X.t"], bk, scale=0.625)
        if t in (RO - 3, RO - 2):
            for k in range(2):
                cp(n("YW"[k]), "G", ap("Y", 1536 * k + j, 1536 * k + 1536, 3), ap("X", 1536 * k + j, 1536 * k + 1536, 3),
                   [n("new%d" % x) for x in range(len(uc) - 1) if uc[x] < 512 * k + 512 and uc[x + 1] > 512 * k], tk("Y%d" % j, 512 * k, 512 * k + 512), n=512)
        if raz:
            if "P" in ue:
                cp(n("gY"), "A", ap("mX", c0, c0 + 160), ind("X", 0, WG, "gl", 32 * m + 20, 32 * m + 30),
                   XT + [n("gl2")], [n("mY")])
            send(n("sY"), ap("lX", c0, c0 + 160), ap("mX", c0, c0 + 160), "ry%d" % m, [n("mY")], [n("lY")])
            cp(n("xX"), "V", ind("X", 0, WW, "sl", 32 * m, 32 * m + 20), ap("lX", 480 * m, 480 * m + 320),
               [n("lX"), n("sl0"), n("sl1")], XT)
            if cfg["xy"] == "V":
                cp(n("xY"), "V", ind("X", 0, WW, "sl", 32 * m + 20, 32 * m + 30), ap("lX", c0, c0 + 160), [n("lY"), n("sl2")], XT)
            else:
                act(n("xY"), ind("X", 0, WW, "sl", 32 * m + 20, 32 * m + 30), ap("lX", c0, c0 + 160), ACT.Tanh, [n("lY"), n("sl2")], XT)
            cp(n("xXt"), "A", ap("X", L, WE), ap("X", 0, TL), tk("X", 0, 64), ["X.t"])

    lists(0)
    for t in range(RO):
        control(t)
        if t % 3 == 2 and t < RO - 1:
            razor_control(t)
        signal(t)
    act("ycs", ap("ycs", 0, 192), ps(SR, 192), ACT.Identity, ["yc"], ["ycs"], [7], bias=QS)
    store("stC", lambda T: T.yc[:], ap("ycs", 0, 192), ["ycs"])
    pe, back = ap("P", 64 * RO, 64 * RO + 64), QS * (RO - 1)
    ts("pq", ap("pq", 0, 64), pe, 16.0 * L - back, -16.0 * L, ALU.is_ge, ALU.mult, ["P12"], ["pq"])
    tt("pw0", ap("pw", 0, 64), pe, ap("pq", 0, 64), ALU.add, ["P12", "pq"], ["pw0"])
    ts("pw1", ap("pw", 64, 128), ap("pw", 0, 64), back, None, ALU.add, None, ["pw0"], ["pw1"])
    ts("pi", ap("pi", 0, 64), ap("pw", 64, 128), 8, None, ALU.arith_shift_right, None, ["pw1"], ["pi0"])
    ts("pi", ap("pi", 64, 128), ap("pw", 64, 128), 255, None, ALU.bitwise_and, None, ["pw1"], ["pi1"])
    cp("pf", "V", ap("pf", 0, 128), ap("pi", 0, 128), ["pi0", "pi1"], ["pf"])
    store("stP", lambda T: T.yp[:], ap("pf", 0, 128), ["pf"])
    return ops


def sequence(ops, head, cycle, last):
    seq = head.split()
    for base, names in ((0, cycle), (3, cycle), (6, cycle), (9, last)):
        for e in names.split():
            i = max(e.find("+"), e.find("-"))
            seq.append(e if i < 0 else "%s.%d" % (e[:i], base + int(e[i:])))
    return [e for e in seq if e in ops]


def waits(ops, seq):
    count, mark, snap, clock, out, bank, place = {}, {}, {}, {}, {}, {}, {}
    for n in seq:
        op = ops[n]
        place[n] = len(place)
        deps = set(x for x in op["deps"] if op["eng"] != "P" or ops[x]["eng"] != "P")
        for b in op["b"]:
            st = bank.setdefault(b, [op["eng"], [], []])
            if st[0] != op["eng"]:
                st[0], st[2], st[1] = op["eng"], st[1], []
            deps.update(st[2])
            st[1].append(n)
        ck = clock.setdefault(op["eng"], {})
        need = {}
        for x in deps:
            s, v = (ops[x]["dma"][2], 16) if x in op["left"] else mark[x]
            if need.get(s, (0, 0))[0] < v:
                need[s] = (v, x)
        ws = []
        for s, (v, x) in sorted(need.items(), key=lambda e: -place[e[1][1]]):
            if ck.get(s, 0) < v:
                ws.append((s, v))
                for s2, v2 in ({s: v} if x in op["left"] else snap[x]).items():
                    if ck.get(s2, 0) < v2:
                        ck[s2] = v2
        out[n] = ws
        s, step = (op["dma"][1], 16) if op["dma"] else (op["eng"], 1)
        count[s] = count.get(s, 0) + step
        mark[n] = (s, count[s])
        if op["dma"] and op["dma"][0] == "remote":
            snap[n] = {s: count[s]}
            count[op["dma"][2]] = count.get(op["dma"][2], 0) + 16
        else:
            snap[n] = dict(ck)
            snap[n][s] = count[s]
    return out, count


CACHE = {}


def emit(g, T, nx):
    if "p" not in CACHE:
        ops = plan(CFG)
        seq = sequence(ops, HEAD, CYCLE, LAST)
        CACHE["p"] = (ops, seq) + waits(ops, seq)
    ops, seq, ws, count = CACHE["p"]
    qs = {"V": g.vector, "A": g.scalar, "P": g.tensor, "G": g, "S": g.sync}
    for n in seq:
        op = ops[n]
        for s, v in ws[n]:
            qs[op["eng"]].wait_ge(T.sem[s], v)
        for fn in op["fn"]:
            ins = fn(g, T, nx)
        if not op["dma"]:
            ins.then_inc(T.sem[op["eng"]], 1)
        elif op["dma"][0] == "local":
            ins.then_inc(T.sem[op["dma"][1]], 16)
    for s in [x for x in count if x[:4] == "left"] + ["V", "A", "P", "G", "sent", "st"]:
        g.wait_ge(T.sem[s], count[s])


def rank_program(g, core, T, topo):
    rank = T.rank_of(core)
    if rank is None:
        return
    nxt = T.cores[(rank + 1) % len(T.cores)]
    rid, pid, se = topo.addr(nxt)
    emit(g, T, (pid, rid, topo.mask(core, nxt)))
